import numpy as np
import ml_dtypes


def mxq(x, axis, fmt="e4m3"):
    dtype, down = {"e4m3": (ml_dtypes.float8_e4m3fn, 7), "e5m2": (ml_dtypes.float8_e5m2, 14)}[fmt]
    v = np.moveaxis(np.asarray(x, np.float32).astype(ml_dtypes.bfloat16).astype(np.float64), axis, -1)
    blocks = v.reshape(v.shape[:-1] + (-1, 32))
    amax = np.abs(blocks).max(-1, keepdims=True)
    byte = np.maximum(np.where(amax > 0, np.frexp(amax)[1] - 1 + 127, 0) - down, 1)
    scale = np.exp2(byte - 127.0)
    codes = (blocks / scale).astype(np.float32).astype(dtype).astype(np.float64)
    return np.moveaxis((codes * scale).reshape(v.shape), -1, axis)


WIDE = False


def mx_kscale(k):
    if not WIDE:
        return np.ones(k)
    levels = np.array([10, -10, 5, -5, 0])
    if k % 512:
        return np.exp2(np.random.permutation(np.resize(levels, k // 32))).repeat(32)
    a = np.empty((k // 512, 16))
    for p in range(k // 512):
        a[p, :8] = np.random.permutation(np.resize(levels, 8))
        for g in range(8):
            far = levels[np.abs(levels - a[p, g]) >= 10]
            a[p, g + 8] = far[np.random.randint(len(far))]
    return np.exp2(a.ravel()).repeat(32)


def f64(x):
    return np.asarray(x).astype(np.float64)


def striped(idx):
    return np.tile(np.asarray(idx).reshape(-1, 16).T, (8, 1)).astype(np.uint16)


def unstriped(offs):
    return offs[:16].T.reshape(-1).astype(np.int64)


E2M1 = np.array([0.0, 0.5, 1.0, 1.5, 2.0, 3.0, 4.0, 6.0, -0.0, -0.5, -1.0, -1.5, -2.0, -3.0, -4.0, -6.0])


def pack_weight(w, fmt):
    k, n = w.shape
    w = f64(np.asarray(w, np.float32).astype(ml_dtypes.bfloat16)).reshape(k // 32, 32, n)
    amax = np.abs(w).max(1)
    if fmt == "e4m3":
        byte = np.frexp(amax)[1] - 1 + 127 - 7
    else:
        mant, ex = np.frexp(amax / 6.0)
        byte = np.where(mant > 0.5, ex, ex - 1) + 127
    byte = np.clip(np.where(amax > 0, byte, 1), 1, 254)
    scaled = (w * np.exp2(127.0 - byte)[:, None, :]).reshape(k, n).astype(np.float32)
    by_word = np.ascontiguousarray(scaled.reshape(k // 512, 128, 4, n).transpose(0, 1, 3, 2))
    if fmt == "e4m3":
        words = by_word.astype(ml_dtypes.float8_e4m3fn).view(np.uint8)
    else:
        c = by_word.astype(ml_dtypes.float4_e2m1fn).view(np.uint8) & 0xF
        words = (c[..., 0::2] | (c[..., 1::2] << 4)).reshape(k // 512, 128, 2 * n)
    return np.ascontiguousarray(words), np.ascontiguousarray(byte.astype(np.uint8).reshape(k // 512, 16, n))


def unpack_weight(words, scales, fmt):
    g, _, n = scales.shape
    words = np.ascontiguousarray(words).reshape(g, 128, n, -1)
    if fmt == "e4m3":
        vals = words.view(ml_dtypes.float8_e4m3fn).astype(np.float64)
    else:
        nib = np.empty((g, 128, n, 4), np.uint8)
        nib[..., 0::2] = words & 0xF
        nib[..., 1::2] = words >> 4
        vals = E2M1[nib]
    vals = vals * np.repeat(np.exp2(scales.astype(np.float64) - 127.0), 8, axis=1)[..., None]
    return vals.transpose(0, 1, 3, 2).reshape(g * 512, n)


B, N, T, D, DV, NQ = 1, 1024, 4096, 512, 128, 256
PAGE = 512


def setup_inputs():
    n = np.random.standard_normal
    pages = np.random.permutation(T // PAGE)[:B * N // PAGE]
    idx = (pages[:, None] * PAGE + np.arange(PAGE)[None, :]).reshape(-1)
    s = mx_kscale(D)[:, None]
    u = np.ones(T)
    u[idx] = mx_kscale(B * N)
    r = np.random.uniform(0.5, 2.0, T)
    k = n((D, T)) / s
    v = n((DV, T)) / (u * r)
    kp = pack_weight(k, "e4m3")
    vp = pack_weight(v.T, "e4m3")
    return {
        "qT": (n((B, D, NQ)) * s * (1.00 / np.sqrt(D))).astype(np.float32),
        "k_words": kp[0],
        "k_scales": kp[1],
        "v_words": vp[0],
        "v_scales": vp[1],
        "vs": np.tile(u * r, (128, 1)).astype(np.float32),
        "og": n((B, NQ, DV)).astype(np.float32),
        "offs": striped(idx),
        "voffs": striped((pages[:, None] * DV + np.arange(DV)[None, :]).reshape(-1)),
    }


def reference(qT, k_words, k_scales, v_words, v_scales, vs, og, offs, voffs):
    idx = unstriped(offs)
    k = unpack_weight(k_words, k_scales, "e4m3")
    v = unpack_weight(v_words, v_scales, "e4m3")
    v = v.reshape(T // 512, 512, DV)[unstriped(voffs)[::DV] // DV].reshape(B, N, DV)
    pick = lambda x: x[:, idx].reshape(x.shape[0], B, N).transpose(1, 0, 2)
    q = f64(qT)
    score = mxq(q, 1, "e4m3").transpose(0, 2, 1) @ pick(k)
    p = np.square(np.maximum(score, 0.0))
    total = p.sum(-1, keepdims=True) + 1.0
    w = p * pick(f64(vs))[:, :1, :]
    y = mxq(w, 2, "e4m3") @ v
    y = y / total
    y = y / (1.0 + np.exp(-f64(og)))
    return y

@@ -1,0 +1,165 @@
+from contextlib import ExitStack
+
+import concourse.mybir as mybir
+from concourse.masks import make_identity
+
+F32 = mybir.dt.float32
+BF16 = mybir.dt.bfloat16
+I32 = mybir.dt.int32
+U32 = mybir.dt.uint32
+U16 = mybir.dt.uint16
+U8 = mybir.dt.uint8
+FP8X4 = mybir.dt.float8_e4m3fn_x4
+ACT = mybir.ActivationFunctionType
+ALU = mybir.AluOpType
+
+P = 128
+PACK = 4
+N, T, D, DV, NQ = 1024, 4096, 512, 128, 256
+PAGE = 512
+PAGES = N // PAGE
+POOL_PAGES = T // PAGE
+HALVES = NQ // P
+LIST_COLS = PAGE // 16
+VS_ROW = 16
+
+FLOPS = 2 * NQ * N * D + 2 * NQ * N * DV
+
+
+def tile_attend_pkv8_rel2_gate_kernel(
+    tc, qT, k_words, k_scales, v_words, v_scales, vs, og, offs, voffs, out
+):
+    nc = tc.nc
+    with ExitStack() as ctx:
+        keep = ctx.enter_context(tc.tile_pool(name="keep", bufs=1))
+        psum = ctx.enter_context(tc.psum_pool(name="psum", bufs=1))
+
+        key_list = keep.tile([P, N // 16], U16, name="key_list")
+        val_list = keep.tile([P, PAGES * DV // 16], U16, name="val_list")
+        kw_pool = keep.tile([P, T], I32, name="kw_pool", tag="kw_pool", align_bytes=64)
+        ks_pool = keep.tile([P, T], U8, name="ks_pool", tag="ks_pool", align_bytes=64)
+        vw_pool = keep.tile([P, POOL_PAGES * DV], I32, name="vw_pool", tag="vw_pool", align_bytes=64)
+        vsc_pool = keep.tile([P, POOL_PAGES * DV], U8, name="vsc_pool", align_bytes=64)
+        ts_pool = keep.tile([P, T], F32, name="ts_pool", tag="ts_pool", align_bytes=64)
+        q_raw = keep.tile([P, PACK, NQ], F32, name="q_raw")
+        og_raw = keep.tile([P, HALVES, DV], F32, name="og_raw")
+        ident = keep.tile([P, P], F32, name="ident")
+
+        nc.vector.memset(ks_pool[:].bitcast(I32), 0)
+        nc.vector.memset(ts_pool[:].bitcast(I32), 0)
+        nc.vector.memset(vsc_pool[:].bitcast(I32), 0)
+        make_identity(nc, ident[:])
+
+        nc.sync.dma_start(key_list[:], offs)
+        nc.sync.dma_start(val_list[:], voffs)
+        nc.sync.dma_start(out=q_raw[:], in_=qT[0].rearrange("(p j) q -> p j q", j=PACK))
+        nc.sync.dma_start(out=og_raw[:], in_=og[0].rearrange("(h p) e -> p h e", p=P))
+        nc.sync.dma_start(out=kw_pool[:], in_=k_words[0].rearrange("p t r -> p (t r)").bitcast(I32))
+        nc.sync.dma_start(
+            out=vw_pool[:].rearrange("p (u e) -> p u e", u=POOL_PAGES),
+            in_=v_words.rearrange("u p e r -> p u (e r)").bitcast(I32),
+        )
+        for quad in range(4):
+            nc.scalar.dma_start(
+                out=ks_pool[32 * quad : 32 * quad + 4, :].bitcast(I32),
+                in_=k_scales[0, 4 * quad : 4 * quad + 4, :].bitcast(I32),
+            )
+        nc.scalar.dma_start(out=ts_pool[VS_ROW : VS_ROW + 1, :], in_=vs[0:1, :])
+        for quad in range(4):
+            nc.sync.dma_start(
+                out=vsc_pool[32 * quad : 32 * quad + 4, :].bitcast(I32).rearrange("p (u e) -> p u e", u=POOL_PAGES),
+                in_=v_scales[:, 4 * quad : 4 * quad + 4, :].rearrange("u f e -> f u e").bitcast(I32),
+            )
+
+        q_bf = [keep.tile([P, P, PACK], BF16, name="q_bf%d" % h, align_bytes=64) for h in range(HALVES)]
+        q_codes = [keep.tile([P, P], U32, name="q_codes%d" % h, align_bytes=64) for h in range(HALVES)]
+        q_scales = [keep.tile([P, P], U8, name="q_scales%d" % h, align_bytes=64) for h in range(HALVES)]
+        for h in range(HALVES):
+            nc.scalar.copy(
+                q_bf[h][:].rearrange("p (c i) j -> p c j i", i=4),
+                q_raw[:, :, h * P : (h + 1) * P].rearrange("p j (c i) -> p c j i", i=4),
+            )
+            nc.vector.quantize_mx(
+                out=q_codes[h][:].bitcast(FP8X4), scales=q_scales[h][:], in_=q_bf[h][:].rearrange("p q j -> p (q j)")
+            )
+        gate = keep.tile([P, HALVES, DV], F32, name="gate")
+        nc.scalar.activation(gate[:], og_raw[:], ACT.Sigmoid)
+
+        ks = keep.tile([P, N], U8, name="ks", align_bytes=64)
+        nc.vector.tensor_copy(ks[:], ks_pool[:].indirect(key_list[:]))
+        ts_row = keep.tile([P, N], F32, name="ts_row", tag="ks_pool", align_bytes=64)
+        nc.vector.tensor_copy(ts_row[:], ts_pool[:].indirect(key_list[:]))
+        ts_col = keep.tile([P, PAGES, PACK], F32, name="ts_col")
+        for g in range(PAGES):
+            turned = psum.tile([P, PACK, P], F32, name="turned", tag="turn%d" % (2 + g))
+            for r in range(PACK):
+                nc.tensor.transpose(turned[:, r, :], ts_row[:, g * PAGE + r : (g + 1) * PAGE : PACK], ident[:])
+            nc.scalar.copy(ts_col[:, g, :], turned[:, :, VS_ROW])
+
+        kw = keep.tile([P, N], U32, name="kw", tag="ts_pool", align_bytes=64)
+        for g in range(PAGES):
+            nc.vector.tensor_copy(
+                kw[:, g * PAGE : (g + 1) * PAGE],
+                kw_pool[:].bitcast(U32).indirect(key_list[:, g * LIST_COLS : (g + 1) * LIST_COLS]),
+            )
+
+        vw = keep.tile([P, PAGES * DV], U32, name="vw", tag="kw_pool", align_bytes=64)
+        vsc = keep.tile([P, PAGES * DV], U8, name="vsc", tag="vw_pool", align_bytes=64)
+        nc.vector.tensor_copy(vw[:], vw_pool[:].bitcast(U32).indirect(val_list[:]))
+        nc.vector.tensor_copy(vsc[:], vsc_pool[:].indirect(val_list[:]))
+
+        sums = keep.tile([P, HALVES, PAGES], F32, name="sums")
+        steps = [(h, g) for g in range(PAGES) for h in range(HALVES)]
+        w_codes = {}
+        w_scales = {}
+        for i, (h, g) in enumerate(steps):
+            score = psum.tile([P, PAGE], F32, name="score", tag="score%d" % i)
+            nc.tensor.matmul_mx(
+                out=score[:],
+                lhsT=q_codes[h][:].bitcast(FP8X4),
+                lhsT_scale=q_scales[h][:],
+                rhs=kw[:, g * PAGE : (g + 1) * PAGE].bitcast(FP8X4),
+                rhs_scale=ks[:, g * PAGE : (g + 1) * PAGE],
+                start=True,
+                stop=True,
+            )
+            pos = keep.tile([P, PACK, P], F32, name="pos%d" % i)
+            nc.scalar.activation(pos[:], score[:].rearrange("p (s r) -> p r s", r=PACK), ACT.Relu)
+            weight = keep.tile([P, PACK, P], F32, name="weight%d" % i)
+            nc.scalar.activation(weight[:], pos[:], ACT.Square, accum_out=sums[:, h, g : g + 1])
+            turned = psum.tile([P, PACK, P], F32, name="turned", tag="turn%d" % i)
+            for r in range(PACK):
+                nc.tensor.transpose(turned[:, r, :], weight[:, r, :], ident[:])
+            w_bf = keep.tile([P, P, PACK], BF16, name="w_bf%d" % i, align_bytes=64)
+            nc.vector.tensor_tensor(
+                w_bf[:],
+                turned[:].rearrange("p r q -> p q r"),
+                ts_col[:, g, :].unsqueeze(1).to_broadcast([P, P, PACK]),
+                ALU.mult,
+            )
+            w_codes[h, g] = keep.tile([P, P], U32, name="w_codes%d" % i, align_bytes=64)
+            w_scales[h, g] = keep.tile([P, P], U8, name="w_scales%d" % i, align_bytes=64)
+            nc.vector.quantize_mx(
+                out=w_codes[h, g][:].bitcast(FP8X4),
+                scales=w_scales[h, g][:],
+                in_=w_bf[:].rearrange("p q r -> p (q r)"),
+            )
+            if g == PAGES - 1:
+                total = keep.tile([P, 1], F32, name="total%d" % h)
+                nc.vector.tensor_scalar(total[:], sums[:, h, 0:1], sums[:, h, 1:2], 1.0, ALU.add, ALU.add)
+                inverse = keep.tile([P, 1], F32, name="inverse%d" % h)
+                nc.vector.reciprocal(inverse[:], total[:])
+                acc = psum.tile([P, DV], F32, name="acc", tag="score%d" % h)
+                for u in range(PAGES):
+                    nc.tensor.matmul_mx(
+                        out=acc[:],
+                        lhsT=w_codes[h, u][:].bitcast(FP8X4),
+                        lhsT_scale=w_scales[h, u][:],
+                        rhs=vw[:, u * DV : (u + 1) * DV].bitcast(FP8X4),
+                        rhs_scale=vsc[:, u * DV : (u + 1) * DV],
+                        start=(u == 0),
+                        stop=(u == PAGES - 1),
+                    )
+                result = keep.tile([P, DV], F32, name="result%d" % h)
+                nc.vector.scalar_tensor_tensor(result[:], acc[:], inverse[:], gate[:, h, :], ALU.mult, ALU.mult)
+                nc.sync.dma_start(out=out[0, h * P : (h + 1) * P, :], in_=result[:])

@@ -21,7 +21,9 @@ PAGES = N // PAGE
 POOL_PAGES = T // PAGE
 HALVES = NQ // P
 LIST_COLS = PAGE // 16
-VS_ROW = 16
+VS_ROW = P - 1
+KS_SPLIT = 768
+TS_SPLIT = 2048
 
 FLOPS = 2 * NQ * N * D + 2 * NQ * N * DV
 
@@ -36,125 +38,133 @@ def tile_attend_pkv8_rel2_gate_kernel(
 
         key_list = keep.tile([P, N // 16], U16, name="key_list")
         val_list = keep.tile([P, PAGES * DV // 16], U16, name="val_list")
-        kw_pool = keep.tile([P, T], I32, name="kw_pool", tag="kw_pool", align_bytes=64)
-        ks_pool = keep.tile([P, T], U8, name="ks_pool", tag="ks_pool", align_bytes=64)
+        kw_pool = keep.tile([P, T], I32, name="kw_pool", align_bytes=64)
+        ks_pool = keep.tile([P, T], U8, name="ks_pool", align_bytes=64)
         vw_pool = keep.tile([P, POOL_PAGES * DV], I32, name="vw_pool", tag="vw_pool", align_bytes=64)
         vsc_pool = keep.tile([P, POOL_PAGES * DV], U8, name="vsc_pool", align_bytes=64)
-        ts_pool = keep.tile([P, T], F32, name="ts_pool", tag="ts_pool", align_bytes=64)
+        ts_pool = keep.tile([P, T], F32, name="ts_pool", align_bytes=64)
         q_raw = keep.tile([P, PACK, NQ], F32, name="q_raw")
         og_raw = keep.tile([P, HALVES, DV], F32, name="og_raw")
         ident = keep.tile([P, P], F32, name="ident")
 
-        nc.vector.memset(ks_pool[:].bitcast(I32), 0)
-        nc.vector.memset(ts_pool[:].bitcast(I32), 0)
-        nc.vector.memset(vsc_pool[:].bitcast(I32), 0)
+        nc.gpsimd.memset(ks_pool[:].bitcast(I32)[:, :KS_SPLIT], 0)
+        nc.vector.memset(ks_pool[:].bitcast(I32)[:, KS_SPLIT:], 0)
+        nc.vector.memset(ts_pool[:VS_ROW, :TS_SPLIT], 0.0)
+        nc.gpsimd.memset(ts_pool[:VS_ROW, TS_SPLIT:], 0.0)
+        nc.gpsimd.memset(vsc_pool[:].bitcast(I32), 0)
         make_identity(nc, ident[:])
 
         nc.sync.dma_start(key_list[:], offs)
-        nc.sync.dma_start(val_list[:], voffs)
+        nc.sync.dma_start(out=ts_pool[VS_ROW:, :], in_=vs[0:1, :])
         nc.sync.dma_start(out=q_raw[:], in_=qT[0].rearrange("(p j) q -> p j q", j=PACK))
-        nc.sync.dma_start(out=og_raw[:], in_=og[0].rearrange("(h p) e -> p h e", p=P))
+        for quad in range(4):
+            nc.sync.dma_start(
+                out=ks_pool[32 * quad : 32 * quad + 4, :].bitcast(I32),
+                in_=k_scales[0, 4 * quad : 4 * quad + 4, :].bitcast(I32),
+            )
         nc.sync.dma_start(out=kw_pool[:], in_=k_words[0].rearrange("p t r -> p (t r)").bitcast(I32))
+        nc.sync.dma_start(val_list[:], voffs)
+        nc.sync.dma_start(out=og_raw[:], in_=og[0].rearrange("(h p) e -> p h e", p=P))
         nc.sync.dma_start(
             out=vw_pool[:].rearrange("p (u e) -> p u e", u=POOL_PAGES),
             in_=v_words.rearrange("u p e r -> p u (e r)").bitcast(I32),
         )
-        for quad in range(4):
-            nc.scalar.dma_start(
-                out=ks_pool[32 * quad : 32 * quad + 4, :].bitcast(I32),
-                in_=k_scales[0, 4 * quad : 4 * quad + 4, :].bitcast(I32),
-            )
-        nc.scalar.dma_start(out=ts_pool[VS_ROW : VS_ROW + 1, :], in_=vs[0:1, :])
         for quad in range(4):
             nc.sync.dma_start(
                 out=vsc_pool[32 * quad : 32 * quad + 4, :].bitcast(I32).rearrange("p (u e) -> p u e", u=POOL_PAGES),
                 in_=v_scales[:, 4 * quad : 4 * quad + 4, :].rearrange("u f e -> f u e").bitcast(I32),
             )
 
-        q_bf = [keep.tile([P, P, PACK], BF16, name="q_bf%d" % h, align_bytes=64) for h in range(HALVES)]
-        q_codes = [keep.tile([P, P], U32, name="q_codes%d" % h, align_bytes=64) for h in range(HALVES)]
-        q_scales = [keep.tile([P, P], U8, name="q_scales%d" % h, align_bytes=64) for h in range(HALVES)]
-        for h in range(HALVES):
-            nc.scalar.copy(
-                q_bf[h][:].rearrange("p (c i) j -> p c j i", i=4),
-                q_raw[:, :, h * P : (h + 1) * P].rearrange("p j (c i) -> p c j i", i=4),
-            )
-            nc.vector.quantize_mx(
-                out=q_codes[h][:].bitcast(FP8X4), scales=q_scales[h][:], in_=q_bf[h][:].rearrange("p q j -> p (q j)")
-            )
-        gate = keep.tile([P, HALVES, DV], F32, name="gate")
-        nc.scalar.activation(gate[:], og_raw[:], ACT.Sigmoid)
-
+        ts_row = keep.tile([P, N], F32, name="ts_row")
+        nc.vector.tensor_copy(ts_row[:], ts_pool[:].indirect(key_list[:]))
         ks = keep.tile([P, N], U8, name="ks", align_bytes=64)
         nc.vector.tensor_copy(ks[:], ks_pool[:].indirect(key_list[:]))
-        ts_row = keep.tile([P, N], F32, name="ts_row", tag="ks_pool", align_bytes=64)
-        nc.vector.tensor_copy(ts_row[:], ts_pool[:].indirect(key_list[:]))
+        q_bf = keep.tile([P, NQ, PACK], BF16, name="q_bf", align_bytes=64)
+        q_codes = keep.tile([P, NQ], U32, name="q_codes", align_bytes=64)
+        q_scales = keep.tile([P, NQ], U8, name="q_scales", align_bytes=64)
+        nc.scalar.activation(
+            q_bf[:].rearrange("p (c i) j -> p c j i", i=4),
+            q_raw[:].rearrange("p j (c i) -> p c j i", i=4),
+            ACT.Copy,
+        )
+        nc.vector.quantize_mx(
+            out=q_codes[:].bitcast(FP8X4), scales=q_scales[:], in_=q_bf[:].rearrange("p q j -> p (q j)")
+        )
         ts_col = keep.tile([P, PAGES, PACK], F32, name="ts_col")
         for g in range(PAGES):
             turned = psum.tile([P, PACK, P], F32, name="turned", tag="turn%d" % (2 + g))
             for r in range(PACK):
                 nc.tensor.transpose(turned[:, r, :], ts_row[:, g * PAGE + r : (g + 1) * PAGE : PACK], ident[:])
-            nc.scalar.copy(ts_col[:, g, :], turned[:, :, VS_ROW])
+            nc.scalar.activation(ts_col[:, g, :], turned[:, :, VS_ROW], ACT.Copy)
 
-        kw = keep.tile([P, N], U32, name="kw", tag="ts_pool", align_bytes=64)
+        kw = keep.tile([P, N], U32, name="kw", align_bytes=64)
         for g in range(PAGES):
             nc.vector.tensor_copy(
                 kw[:, g * PAGE : (g + 1) * PAGE],
                 kw_pool[:].bitcast(U32).indirect(key_list[:, g * LIST_COLS : (g + 1) * LIST_COLS]),
             )
 
-        vw = keep.tile([P, PAGES * DV], U32, name="vw", tag="kw_pool", align_bytes=64)
-        vsc = keep.tile([P, PAGES * DV], U8, name="vsc", tag="vw_pool", align_bytes=64)
+        gate = keep.tile([P, HALVES, DV], F32, name="gate")
+        half_tanh = keep.tile([P, HALVES, DV], F32, name="half_tanh")
+        nc.scalar.activation(half_tanh[:], og_raw[:], ACT.Tanh, scale=0.5)
+        nc.scalar.activation(gate[:], half_tanh[:], ACT.Copy, scale=0.5, bias=0.5)
+        vw = keep.tile([P, PAGES * DV], U32, name="vw", align_bytes=64)
+        vsc = keep.tile([P, PAGES * DV], U8, name="vsc", align_bytes=64)
         nc.vector.tensor_copy(vw[:], vw_pool[:].bitcast(U32).indirect(val_list[:]))
         nc.vector.tensor_copy(vsc[:], vsc_pool[:].indirect(val_list[:]))
 
         sums = keep.tile([P, HALVES, PAGES], F32, name="sums")
         steps = [(h, g) for g in range(PAGES) for h in range(HALVES)]
-        w_codes = {}
-        w_scales = {}
+        w_bf = [keep.tile([P, NQ, PACK], BF16, name="w_bf%d" % g, align_bytes=64) for g in range(PAGES)]
+        w_codes = [keep.tile([P, NQ], U32, name="w_codes%d" % g, align_bytes=64) for g in range(PAGES)]
+        w_scales = [keep.tile([P, NQ], U8, name="w_scales%d" % g, align_bytes=64) for g in range(PAGES)]
         for i, (h, g) in enumerate(steps):
             score = psum.tile([P, PAGE], F32, name="score", tag="score%d" % i)
             nc.tensor.matmul_mx(
                 out=score[:],
-                lhsT=q_codes[h][:].bitcast(FP8X4),
-                lhsT_scale=q_scales[h][:],
+                lhsT=q_codes[:, h * P : (h + 1) * P].bitcast(FP8X4),
+                lhsT_scale=q_scales[:, h * P : (h + 1) * P],
                 rhs=kw[:, g * PAGE : (g + 1) * PAGE].bitcast(FP8X4),
                 rhs_scale=ks[:, g * PAGE : (g + 1) * PAGE],
                 start=True,
                 stop=True,
             )
-            pos = keep.tile([P, PACK, P], F32, name="pos%d" % i)
-            nc.scalar.activation(pos[:], score[:].rearrange("p (s r) -> p r s", r=PACK), ACT.Relu)
+            if i == 2:
+                pos = keep.tile([P, PACK, P], F32, name="pos2", tag="vw_pool", align_bytes=64)
+                nc.vector.tensor_scalar(pos[:], score[:].rearrange("p (s r) -> p r s", r=PACK), 0.0, None, ALU.max)
+            else:
+                pos = keep.tile([P, PACK, P], F32, name="pos%d" % i)
+                nc.scalar.activation(pos[:], score[:].rearrange("p (s r) -> p r s", r=PACK), ACT.Relu)
             weight = keep.tile([P, PACK, P], F32, name="weight%d" % i)
             nc.scalar.activation(weight[:], pos[:], ACT.Square, accum_out=sums[:, h, g : g + 1])
             turned = psum.tile([P, PACK, P], F32, name="turned", tag="turn%d" % i)
             for r in range(PACK):
                 nc.tensor.transpose(turned[:, r, :], weight[:, r, :], ident[:])
-            w_bf = keep.tile([P, P, PACK], BF16, name="w_bf%d" % i, align_bytes=64)
             nc.vector.tensor_tensor(
-                w_bf[:],
+                w_bf[g][:, h * P : (h + 1) * P, :],
                 turned[:].rearrange("p r q -> p q r"),
                 ts_col[:, g, :].unsqueeze(1).to_broadcast([P, P, PACK]),
                 ALU.mult,
             )
-            w_codes[h, g] = keep.tile([P, P], U32, name="w_codes%d" % i, align_bytes=64)
-            w_scales[h, g] = keep.tile([P, P], U8, name="w_scales%d" % i, align_bytes=64)
-            nc.vector.quantize_mx(
-                out=w_codes[h, g][:].bitcast(FP8X4),
-                scales=w_scales[h, g][:],
-                in_=w_bf[:].rearrange("p q r -> p (q r)"),
-            )
+            if g == PAGES - 1 or h == HALVES - 1:
+                rows = slice(h * P, (h + 1) * P) if g == PAGES - 1 else slice(0, NQ)
+                plane = w_scales[g]
+                nc.vector.quantize_mx(
+                    out=w_codes[g][:, rows].bitcast(FP8X4),
+                    scales=plane[:, rows],
+                    in_=w_bf[g][:, rows, :].rearrange("p q r -> p (q r)"),
+                )
             if g == PAGES - 1:
                 total = keep.tile([P, 1], F32, name="total%d" % h)
-                nc.vector.tensor_scalar(total[:], sums[:, h, 0:1], sums[:, h, 1:2], 1.0, ALU.add, ALU.add)
+                nc.gpsimd.tensor_scalar(total[:], sums[:, h, 0:1], sums[:, h, 1:2], 1.0, ALU.add, ALU.add)
                 inverse = keep.tile([P, 1], F32, name="inverse%d" % h)
                 nc.vector.reciprocal(inverse[:], total[:])
                 acc = psum.tile([P, DV], F32, name="acc", tag="score%d" % h)
                 for u in range(PAGES):
                     nc.tensor.matmul_mx(
                         out=acc[:],
-                        lhsT=w_codes[h, u][:].bitcast(FP8X4),
-                        lhsT_scale=w_scales[h, u][:],
+                        lhsT=w_codes[u][:, h * P : (h + 1) * P].bitcast(FP8X4),
+                        lhsT_scale=w_scales[u][:, h * P : (h + 1) * P],
                         rhs=vw[:, u * DV : (u + 1) * DV].bitcast(FP8X4),
                         rhs_scale=vsc[:, u * DV : (u + 1) * DV],
                         start=(u == 0),

@@ -15,15 +15,16 @@ ALU = mybir.AluOpType
 
 P = 128
 PACK = 4
+QUADS = 4
 N, T, D, DV, NQ = 1024, 4096, 512, 128, 256
 PAGE = 512
 PAGES = N // PAGE
 POOL_PAGES = T // PAGE
-HALVES = NQ // P
-LIST_COLS = PAGE // 16
+BLOCKS = NQ // P
+PAGE_COLS = PAGE // 16
 VS_ROW = P - 1
 KS_SPLIT = 768
-TS_SPLIT = 2048
+VS_SPLIT = 1536
 
 FLOPS = 2 * NQ * N * D + 2 * NQ * N * DV
 
@@ -39,27 +40,29 @@ def tile_attend_pkv8_rel2_gate_kernel(
         key_list = keep.tile([P, N // 16], U16, name="key_list")
         val_list = keep.tile([P, PAGES * DV // 16], U16, name="val_list")
         kw_pool = keep.tile([P, T], I32, name="kw_pool", align_bytes=64)
-        ks_pool = keep.tile([P, T], U8, name="ks_pool", align_bytes=64)
+        ks_pool = keep.tile([P, T + 4], U8, name="ks_pool", align_bytes=64)
         vw_pool = keep.tile([P, POOL_PAGES * DV], I32, name="vw_pool", tag="vw_pool", align_bytes=64)
-        vsc_pool = keep.tile([P, POOL_PAGES * DV], U8, name="vsc_pool", align_bytes=64)
-        ts_pool = keep.tile([P, T], F32, name="ts_pool", align_bytes=64)
+        vsc_pool = keep.tile([P, POOL_PAGES * DV], U8, name="vsc_pool", tag="vsc_pool", align_bytes=64)
+        vs_pool = keep.tile([P, T + 1], F32, name="vs_pool", align_bytes=64)
         q_raw = keep.tile([P, PACK, NQ], F32, name="q_raw")
-        og_raw = keep.tile([P, HALVES, DV], F32, name="og_raw")
+        og_raw = keep.tile([P, BLOCKS, DV], F32, name="og_raw")
         ident = keep.tile([P, P], F32, name="ident")
 
-        nc.gpsimd.memset(ks_pool[:].bitcast(I32)[:, :KS_SPLIT], 0)
-        nc.vector.memset(ks_pool[:].bitcast(I32)[:, KS_SPLIT:], 0)
-        nc.vector.memset(ts_pool[:VS_ROW, :TS_SPLIT], 0.0)
-        nc.gpsimd.memset(ts_pool[:VS_ROW, TS_SPLIT:], 0.0)
+        ks_words = ks_pool[:].bitcast(I32)
+        nc.gpsimd.memset(ks_words[:, :KS_SPLIT], 0)
+        nc.vector.memset(ks_words[:, KS_SPLIT:], 0)
+        nc.gpsimd.memset(ident[:], 0.0)
         nc.gpsimd.memset(vsc_pool[:].bitcast(I32), 0)
-        make_identity(nc, ident[:])
+        make_identity(nc, ident[:], nomemset=True)
+        nc.vector.memset(vs_pool[:VS_ROW, VS_SPLIT:], 0.0)
+        nc.gpsimd.memset(vs_pool[:VS_ROW, :VS_SPLIT], 0.0)
 
         nc.sync.dma_start(key_list[:], offs)
-        nc.sync.dma_start(out=ts_pool[VS_ROW:, :], in_=vs[0:1, :])
-        nc.sync.dma_start(out=q_raw[:], in_=qT[0].rearrange("(p j) q -> p j q", j=PACK))
-        for quad in range(4):
+        nc.sync.dma_start(out=vs_pool[VS_ROW:, :T], in_=vs[0:1, :])
+        nc.sync.dma_start(out=q_raw[:], in_=qT[0].rearrange("(p r) q -> p r q", r=PACK))
+        for quad in range(QUADS):
             nc.sync.dma_start(
-                out=ks_pool[32 * quad : 32 * quad + 4, :].bitcast(I32),
+                out=ks_words[32 * quad : 32 * quad + 4, : T // 4],
                 in_=k_scales[0, 4 * quad : 4 * quad + 4, :].bitcast(I32),
             )
         nc.sync.dma_start(out=kw_pool[:], in_=k_words[0].rearrange("p t r -> p (t r)").bitcast(I32))
@@ -69,57 +72,63 @@ def tile_attend_pkv8_rel2_gate_kernel(
             out=vw_pool[:].rearrange("p (u e) -> p u e", u=POOL_PAGES),
             in_=v_words.rearrange("u p e r -> p u (e r)").bitcast(I32),
         )
-        for quad in range(4):
-            nc.sync.dma_start(
+        for quad in range(QUADS):
+            nc.gpsimd.dma_start(
                 out=vsc_pool[32 * quad : 32 * quad + 4, :].bitcast(I32).rearrange("p (u e) -> p u e", u=POOL_PAGES),
                 in_=v_scales[:, 4 * quad : 4 * quad + 4, :].rearrange("u f e -> f u e").bitcast(I32),
             )
 
-        ts_row = keep.tile([P, N], F32, name="ts_row")
-        nc.vector.tensor_copy(ts_row[:], ts_pool[:].indirect(key_list[:]))
+        vs_row = keep.tile([P, N], F32, name="vs_row")
+        nc.vector.tensor_copy(vs_row[:], vs_pool[:, :T].indirect(key_list[:]))
         ks = keep.tile([P, N], U8, name="ks", align_bytes=64)
-        nc.vector.tensor_copy(ks[:], ks_pool[:].indirect(key_list[:]))
+        nc.vector.tensor_copy(ks[:], ks_pool[:, :T].indirect(key_list[:]))
         q_bf = keep.tile([P, NQ, PACK], BF16, name="q_bf", align_bytes=64)
         q_codes = keep.tile([P, NQ], U32, name="q_codes", align_bytes=64)
         q_scales = keep.tile([P, NQ], U8, name="q_scales", align_bytes=64)
         nc.scalar.activation(
-            q_bf[:].rearrange("p (c i) j -> p c j i", i=4),
-            q_raw[:].rearrange("p j (c i) -> p c j i", i=4),
+            q_bf[:].rearrange("p (c i) r -> p c r i", i=4),
+            q_raw[:].rearrange("p r (c i) -> p c r i", i=4),
             ACT.Copy,
         )
         nc.vector.quantize_mx(
-            out=q_codes[:].bitcast(FP8X4), scales=q_scales[:], in_=q_bf[:].rearrange("p q j -> p (q j)")
+            out=q_codes[:].bitcast(FP8X4), scales=q_scales[:], in_=q_bf[:].rearrange("p q r -> p (q r)")
         )
-        ts_col = keep.tile([P, PAGES, PACK], F32, name="ts_col")
+        vs_col = keep.tile([P, PAGES, PACK], F32, name="vs_col")
         for g in range(PAGES):
-            turned = psum.tile([P, PACK, P], F32, name="turned", tag="turn%d" % (2 + g))
+            vs_turned = psum.tile([P, PACK, P], F32, name="vs_turned", tag="turn%d" % (BLOCKS + g))
             for r in range(PACK):
-                nc.tensor.transpose(turned[:, r, :], ts_row[:, g * PAGE + r : (g + 1) * PAGE : PACK], ident[:])
-            nc.scalar.activation(ts_col[:, g, :], turned[:, :, VS_ROW], ACT.Copy)
+                nc.tensor.transpose(vs_turned[:, r, :], vs_row[:, g * PAGE + r : (g + 1) * PAGE : PACK], ident[:])
+            nc.scalar.activation(vs_col[:, g, :], vs_turned[:, :, VS_ROW], ACT.Copy)
 
         kw = keep.tile([P, N], U32, name="kw", align_bytes=64)
         for g in range(PAGES):
             nc.vector.tensor_copy(
                 kw[:, g * PAGE : (g + 1) * PAGE],
-                kw_pool[:].bitcast(U32).indirect(key_list[:, g * LIST_COLS : (g + 1) * LIST_COLS]),
+                kw_pool[:].bitcast(U32).indirect(key_list[:, g * PAGE_COLS : (g + 1) * PAGE_COLS]),
             )
 
-        gate = keep.tile([P, HALVES, DV], F32, name="gate")
-        half_tanh = keep.tile([P, HALVES, DV], F32, name="half_tanh")
-        nc.scalar.activation(half_tanh[:], og_raw[:], ACT.Tanh, scale=0.5)
-        nc.scalar.activation(gate[:], half_tanh[:], ACT.Copy, scale=0.5, bias=0.5)
+        gate = keep.tile([P, BLOCKS, DV], F32, name="gate")
+        og_tanh = keep.tile([P, BLOCKS, DV], F32, name="og_tanh")
+        nc.scalar.activation(og_tanh[:], og_raw[:], ACT.Tanh, scale=0.5)
+        nc.scalar.activation(gate[:], og_tanh[:], ACT.Copy, scale=0.5, bias=0.5)
+
         vw = keep.tile([P, PAGES * DV], U32, name="vw", align_bytes=64)
-        vsc = keep.tile([P, PAGES * DV], U8, name="vsc", align_bytes=64)
         nc.vector.tensor_copy(vw[:], vw_pool[:].bitcast(U32).indirect(val_list[:]))
+        vsc = keep.tile([P, PAGES * DV], U8, name="vsc", align_bytes=64)
         nc.vector.tensor_copy(vsc[:], vsc_pool[:].indirect(val_list[:]))
 
-        sums = keep.tile([P, HALVES, PAGES], F32, name="sums")
-        steps = [(h, g) for g in range(PAGES) for h in range(HALVES)]
-        w_bf = [keep.tile([P, NQ, PACK], BF16, name="w_bf%d" % g, align_bytes=64) for g in range(PAGES)]
-        w_codes = [keep.tile([P, NQ], U32, name="w_codes%d" % g, align_bytes=64) for g in range(PAGES)]
-        w_scales = [keep.tile([P, NQ], U8, name="w_scales%d" % g, align_bytes=64) for g in range(PAGES)]
-        for i, (h, g) in enumerate(steps):
-            score = psum.tile([P, PAGE], F32, name="score", tag="score%d" % i)
+        sums = keep.tile([P, BLOCKS, PAGES], F32, name="sums")
+        pos = [
+            keep.tile([P, BLOCKS, PACK, P], F32, name="pos", tag=tag, align_bytes=64)
+            for tag in ("pos_first", "vw_pool")
+        ]
+        w_bf = [
+            keep.tile([P, NQ, PACK], BF16, name="w_bf", tag=tag, align_bytes=64) for tag in ("vsc_pool", "w_last")
+        ]
+
+        def weigh(g, h):
+            step = g * BLOCKS + h
+            score = psum.tile([P, PAGE], F32, name="score", tag="score%d" % step)
             nc.tensor.matmul_mx(
                 out=score[:],
                 lhsT=q_codes[:, h * P : (h + 1) * P].bitcast(FP8X4),
@@ -129,47 +138,60 @@ def tile_attend_pkv8_rel2_gate_kernel(
                 start=True,
                 stop=True,
             )
-            if i == 2:
-                pos = keep.tile([P, PACK, P], F32, name="pos2", tag="vw_pool", align_bytes=64)
-                nc.vector.tensor_scalar(pos[:], score[:].rearrange("p (s r) -> p r s", r=PACK), 0.0, None, ALU.max)
+            dealt = score[:].rearrange("q (s r) -> q r s", r=PACK)
+            if g == 0:
+                nc.scalar.activation(pos[g][:, h], dealt, ACT.Relu)
             else:
-                pos = keep.tile([P, PACK, P], F32, name="pos%d" % i)
-                nc.scalar.activation(pos[:], score[:].rearrange("p (s r) -> p r s", r=PACK), ACT.Relu)
-            weight = keep.tile([P, PACK, P], F32, name="weight%d" % i)
-            nc.scalar.activation(weight[:], pos[:], ACT.Square, accum_out=sums[:, h, g : g + 1])
-            turned = psum.tile([P, PACK, P], F32, name="turned", tag="turn%d" % i)
+                nc.vector.tensor_scalar(pos[g][:, h], dealt, 0.0, None, ALU.max)
+            weight = keep.tile([P, PACK, P], F32, name="weight", tag="weight%d" % step, align_bytes=64)
+            nc.scalar.activation(weight[:], pos[g][:, h], ACT.Square, accum_out=sums[:, h, g : g + 1])
+            turned = psum.tile([P, PACK, P], F32, name="turned", tag="turn%d" % step)
             for r in range(PACK):
                 nc.tensor.transpose(turned[:, r, :], weight[:, r, :], ident[:])
             nc.vector.tensor_tensor(
                 w_bf[g][:, h * P : (h + 1) * P, :],
-                turned[:].rearrange("p r q -> p q r"),
-                ts_col[:, g, :].unsqueeze(1).to_broadcast([P, P, PACK]),
+                turned[:].rearrange("s r q -> s q r"),
+                vs_col[:, g, :].unsqueeze(1).to_broadcast([P, P, PACK]),
                 ALU.mult,
             )
-            if g == PAGES - 1 or h == HALVES - 1:
-                rows = slice(h * P, (h + 1) * P) if g == PAGES - 1 else slice(0, NQ)
-                plane = w_scales[g]
-                nc.vector.quantize_mx(
-                    out=w_codes[g][:, rows].bitcast(FP8X4),
-                    scales=plane[:, rows],
-                    in_=w_bf[g][:, rows, :].rearrange("p q r -> p (q r)"),
+
+        def quantise(g, first, count, tag):
+            codes = keep.tile([P, count], U32, name="w_codes", tag=tag, align_bytes=64)
+            scales = keep.tile([P, count], U8, name="w_scales", tag="scales_" + tag, align_bytes=64)
+            nc.vector.quantize_mx(
+                out=codes[:].bitcast(FP8X4),
+                scales=scales[:],
+                in_=w_bf[g][:, first : first + count, :].rearrange("s q r -> s (q r)"),
+            )
+            return codes, scales
+
+        for h in range(BLOCKS):
+            weigh(0, h)
+        first_codes, first_scales = quantise(0, 0, NQ, "codes_first")
+        for h in range(BLOCKS):
+            weigh(1, h)
+
+        for h, tag in enumerate(("weight%d" % (PAGES * BLOCKS - 1), "codes_last")):
+            last_codes, last_scales = quantise(1, h * P, P, tag)
+            total = keep.tile([P, 1], F32, name="total%d" % h)
+            nc.gpsimd.tensor_scalar(total[:], sums[:, h, 0:1], sums[:, h, 1:2], 1.0, ALU.add, ALU.add)
+            inverse = keep.tile([P, 1], F32, name="inverse%d" % h)
+            nc.vector.reciprocal(inverse[:], total[:])
+            acc = psum.tile([P, DV], F32, name="acc", tag="turn%d" % (BLOCKS + h))
+            operands = [
+                (first_codes[:, h * P : (h + 1) * P], first_scales[:, h * P : (h + 1) * P]),
+                (last_codes[:], last_scales[:]),
+            ]
+            for g, (codes, scales) in enumerate(operands):
+                nc.tensor.matmul_mx(
+                    out=acc[:],
+                    lhsT=codes.bitcast(FP8X4),
+                    lhsT_scale=scales,
+                    rhs=vw[:, g * DV : (g + 1) * DV].bitcast(FP8X4),
+                    rhs_scale=vsc[:, g * DV : (g + 1) * DV],
+                    start=(g == 0),
+                    stop=(g == PAGES - 1),
                 )
-            if g == PAGES - 1:
-                total = keep.tile([P, 1], F32, name="total%d" % h)
-                nc.gpsimd.tensor_scalar(total[:], sums[:, h, 0:1], sums[:, h, 1:2], 1.0, ALU.add, ALU.add)
-                inverse = keep.tile([P, 1], F32, name="inverse%d" % h)
-                nc.vector.reciprocal(inverse[:], total[:])
-                acc = psum.tile([P, DV], F32, name="acc", tag="score%d" % h)
-                for u in range(PAGES):
-                    nc.tensor.matmul_mx(
-                        out=acc[:],
-                        lhsT=w_codes[u][:, h * P : (h + 1) * P].bitcast(FP8X4),
-                        lhsT_scale=w_scales[u][:, h * P : (h + 1) * P],
-                        rhs=vw[:, u * DV : (u + 1) * DV].bitcast(FP8X4),
-                        rhs_scale=vsc[:, u * DV : (u + 1) * DV],
-                        start=(u == 0),
-                        stop=(u == PAGES - 1),
-                    )
-                result = keep.tile([P, DV], F32, name="result%d" % h)
-                nc.vector.scalar_tensor_tensor(result[:], acc[:], inverse[:], gate[:, h, :], ALU.mult, ALU.mult)
-                nc.sync.dma_start(out=out[0, h * P : (h + 1) * P, :], in_=result[:])
+            result = keep.tile([P, DV], F32, name="result%d" % h)
+            nc.vector.scalar_tensor_tensor(result[:], acc[:], inverse[:], gate[:, h, :], ALU.mult, ALU.mult)
+            nc.sync.dma_start(out=out[0, h * P : (h + 1) * P, :], in_=result[:])

@@ -23,7 +23,7 @@ POOL_PAGES = T // PAGE
 BLOCKS = NQ // P
 PAGE_COLS = PAGE // 16
 VS_ROW = P - 1
-KS_SPLIT = 768
+KS_SPLIT = 640
 VS_SPLIT = 1536
 
 FLOPS = 2 * NQ * N * D + 2 * NQ * N * DV
@@ -49,13 +49,13 @@ def tile_attend_pkv8_rel2_gate_kernel(
         ident = keep.tile([P, P], F32, name="ident")
 
         ks_words = ks_pool[:].bitcast(I32)
+        nc.gpsimd.memset(ident[:], 0.0)
         nc.gpsimd.memset(ks_words[:, :KS_SPLIT], 0)
         nc.vector.memset(ks_words[:, KS_SPLIT:], 0)
-        nc.gpsimd.memset(ident[:], 0.0)
-        nc.gpsimd.memset(vsc_pool[:].bitcast(I32), 0)
         make_identity(nc, ident[:], nomemset=True)
         nc.vector.memset(vs_pool[:VS_ROW, VS_SPLIT:], 0.0)
         nc.gpsimd.memset(vs_pool[:VS_ROW, :VS_SPLIT], 0.0)
+        nc.gpsimd.memset(vsc_pool[:].bitcast(I32), 0)
 
         nc.sync.dma_start(key_list[:], offs)
         nc.sync.dma_start(out=vs_pool[VS_ROW:, :T], in_=vs[0:1, :])

@@ -22,9 +22,10 @@ PAGES = N // PAGE
 POOL_PAGES = T // PAGE
 BLOCKS = NQ // P
 PAGE_COLS = PAGE // 16
+SCALE_ROWS = 16
+SCALE_ROW0 = P - SCALE_ROWS
 VS_ROW = P - 1
-KS_SPLIT = 640
-VS_SPLIT = 1536
+VS_SPLIT = 3200
 
 FLOPS = 2 * NQ * N * D + 2 * NQ * N * DV
 
@@ -40,8 +41,7 @@ def tile_attend_pkv8_rel2_gate_kernel(
         key_list = keep.tile([P, N // 16], U16, name="key_list")
         val_list = keep.tile([P, PAGES * DV // 16], U16, name="val_list")
         kw_pool = keep.tile([P, T], I32, name="kw_pool", align_bytes=64)
-        ks_pool = keep.tile([P, T + 4], U8, name="ks_pool", align_bytes=64)
-        vw_pool = keep.tile([P, POOL_PAGES * DV], I32, name="vw_pool", tag="vw_pool", align_bytes=64)
+        ks_pool = keep.tile([P, T + 4], U8, name="ks_pool", tag="ks_pool", align_bytes=64)
         vsc_pool = keep.tile([P, POOL_PAGES * DV], U8, name="vsc_pool", tag="vsc_pool", align_bytes=64)
         vs_pool = keep.tile([P, T + 1], F32, name="vs_pool", align_bytes=64)
         q_raw = keep.tile([P, PACK, NQ], F32, name="q_raw")
@@ -49,39 +49,52 @@ def tile_attend_pkv8_rel2_gate_kernel(
         ident = keep.tile([P, P], F32, name="ident")
 
         ks_words = ks_pool[:].bitcast(I32)
+        vsc_words = vsc_pool[:].bitcast(I32)
+        ks = keep.tile([P, N], U8, name="ks", align_bytes=64)
+        vsc = keep.tile([P, PAGES * DV], U8, name="vsc", align_bytes=64)
+        nc.vector.memset(ks_words[:SCALE_ROW0, :], 0)
         nc.gpsimd.memset(ident[:], 0.0)
-        nc.gpsimd.memset(ks_words[:, :KS_SPLIT], 0)
-        nc.vector.memset(ks_words[:, KS_SPLIT:], 0)
         make_identity(nc, ident[:], nomemset=True)
         nc.vector.memset(vs_pool[:VS_ROW, VS_SPLIT:], 0.0)
         nc.gpsimd.memset(vs_pool[:VS_ROW, :VS_SPLIT], 0.0)
-        nc.gpsimd.memset(vsc_pool[:].bitcast(I32), 0)
+        nc.gpsimd.memset(ks[:].bitcast(I32), 0)
+        nc.gpsimd.memset(vsc_words[:SCALE_ROW0, :], 0)
+        nc.gpsimd.memset(vsc[:].bitcast(I32), 0)
 
         nc.sync.dma_start(key_list[:], offs)
+        nc.sync.dma_start(out=ks_words[SCALE_ROW0:, : T // 4], in_=k_scales[0].bitcast(I32))
         nc.sync.dma_start(out=vs_pool[VS_ROW:, :T], in_=vs[0:1, :])
         nc.sync.dma_start(out=q_raw[:], in_=qT[0].rearrange("(p r) q -> p r q", r=PACK))
-        for quad in range(QUADS):
-            nc.sync.dma_start(
-                out=ks_words[32 * quad : 32 * quad + 4, : T // 4],
-                in_=k_scales[0, 4 * quad : 4 * quad + 4, :].bitcast(I32),
-            )
-        nc.sync.dma_start(out=kw_pool[:], in_=k_words[0].rearrange("p t r -> p (t r)").bitcast(I32))
         nc.sync.dma_start(val_list[:], voffs)
+        nc.sync.dma_start(
+            out=vsc_words[SCALE_ROW0:, :].rearrange("f (u e) -> f u e", u=POOL_PAGES),
+            in_=v_scales.rearrange("u f e -> f u e").bitcast(I32),
+        )
+        nc.sync.dma_start(out=kw_pool[:], in_=k_words[0].rearrange("p t r -> p (t r)").bitcast(I32))
         nc.sync.dma_start(out=og_raw[:], in_=og[0].rearrange("(h p) e -> p h e", p=P))
+
+        def place_scale_rows(plane, gathered):
+            for quad in range(QUADS):
+                first = SCALE_ROW0 + 4 * quad
+                nc.sync.dma_start(
+                    out=plane[32 * quad : 32 * quad + 4, :].bitcast(I32),
+                    in_=gathered[first : first + 4, :].bitcast(I32),
+                )
+
+        ks_rows = keep.tile([P, N], U8, name="ks_rows", align_bytes=64)
+        nc.vector.tensor_copy(ks_rows[:], ks_pool[:, :T].indirect(key_list[:]))
+        place_scale_rows(ks, ks_rows)
+        vw_pool = keep.tile([P, POOL_PAGES * DV], I32, name="vw_pool", tag="ks_pool", align_bytes=64)
         nc.sync.dma_start(
             out=vw_pool[:].rearrange("p (u e) -> p u e", u=POOL_PAGES),
             in_=v_words.rearrange("u p e r -> p u (e r)").bitcast(I32),
         )
-        for quad in range(QUADS):
-            nc.gpsimd.dma_start(
-                out=vsc_pool[32 * quad : 32 * quad + 4, :].bitcast(I32).rearrange("p (u e) -> p u e", u=POOL_PAGES),
-                in_=v_scales[:, 4 * quad : 4 * quad + 4, :].rearrange("u f e -> f u e").bitcast(I32),
-            )
-
         vs_row = keep.tile([P, N], F32, name="vs_row")
-        nc.vector.tensor_copy(vs_row[:], vs_pool[:, :T].indirect(key_list[:]))
-        ks = keep.tile([P, N], U8, name="ks", align_bytes=64)
-        nc.vector.tensor_copy(ks[:], ks_pool[:, :T].indirect(key_list[:]))
+        for g in range(PAGES):
+            nc.vector.tensor_copy(
+                vs_row[:, g * PAGE : (g + 1) * PAGE],
+                vs_pool[:, :T].indirect(key_list[:, g * PAGE_COLS : (g + 1) * PAGE_COLS]),
+            )
         q_bf = keep.tile([P, NQ, PACK], BF16, name="q_bf", align_bytes=64)
         q_codes = keep.tile([P, NQ], U32, name="q_codes", align_bytes=64)
         q_scales = keep.tile([P, NQ], U8, name="q_scales", align_bytes=64)
@@ -93,6 +106,9 @@ def tile_attend_pkv8_rel2_gate_kernel(
         nc.vector.quantize_mx(
             out=q_codes[:].bitcast(FP8X4), scales=q_scales[:], in_=q_bf[:].rearrange("p q r -> p (q r)")
         )
+        vsc_rows = keep.tile([P, PAGES * DV], U8, name="vsc_rows", align_bytes=64)
+        nc.vector.tensor_copy(vsc_rows[:], vsc_pool[:].indirect(val_list[:]))
+        place_scale_rows(vsc, vsc_rows)
         vs_col = keep.tile([P, PAGES, PACK], F32, name="vs_col")
         for g in range(PAGES):
             vs_turned = psum.tile([P, PACK, P], F32, name="vs_turned", tag="turn%d" % (BLOCKS + g))
@@ -114,13 +130,11 @@ def tile_attend_pkv8_rel2_gate_kernel(
 
         vw = keep.tile([P, PAGES * DV], U32, name="vw", align_bytes=64)
         nc.vector.tensor_copy(vw[:], vw_pool[:].bitcast(U32).indirect(val_list[:]))
-        vsc = keep.tile([P, PAGES * DV], U8, name="vsc", align_bytes=64)
-        nc.vector.tensor_copy(vsc[:], vsc_pool[:].indirect(val_list[:]))
 
         sums = keep.tile([P, BLOCKS, PAGES], F32, name="sums")
         pos = [
             keep.tile([P, BLOCKS, PACK, P], F32, name="pos", tag=tag, align_bytes=64)
-            for tag in ("pos_first", "vw_pool")
+            for tag in ("pos_first", "ks_pool")
         ]
         w_bf = [
             keep.tile([P, NQ, PACK], BF16, name="w_bf", tag=tag, align_bytes=64) for tag in ("vsc_pool", "w_last")

@@ -36,16 +36,16 @@ def tile_attend_pkv8_rel2_gate_kernel(
     nc = tc.nc
     with ExitStack() as ctx:
         keep = ctx.enter_context(tc.tile_pool(name="keep", bufs=1))
+        shared = ctx.enter_context(tc.tile_pool(name="shared", bufs=1))
         psum = ctx.enter_context(tc.psum_pool(name="psum", bufs=1))
 
         key_list = keep.tile([P, N // 16], U16, name="key_list")
         val_list = keep.tile([P, PAGES * DV // 16], U16, name="val_list")
         kw_pool = keep.tile([P, T], I32, name="kw_pool", align_bytes=64)
-        ks_pool = keep.tile([P, T + 4], U8, name="ks_pool", tag="ks_pool", align_bytes=64)
+        ks_pool = shared.tile([P, T + 4], U8, name="ks_pool", align_bytes=64, offset=0)
         vsc_pool = keep.tile([P, POOL_PAGES * DV], U8, name="vsc_pool", tag="vsc_pool", align_bytes=64)
         vs_pool = keep.tile([P, T + 1], F32, name="vs_pool", align_bytes=64)
         q_raw = keep.tile([P, PACK, NQ], F32, name="q_raw")
-        og_raw = keep.tile([P, BLOCKS, DV], F32, name="og_raw")
         ident = keep.tile([P, P], F32, name="ident")
 
         ks_words = ks_pool[:].bitcast(I32)
@@ -53,11 +53,11 @@ def tile_attend_pkv8_rel2_gate_kernel(
         ks = keep.tile([P, N], U8, name="ks", align_bytes=64)
         vsc = keep.tile([P, PAGES * DV], U8, name="vsc", align_bytes=64)
         nc.vector.memset(ks_words[:SCALE_ROW0, :], 0)
-        nc.gpsimd.memset(ident[:], 0.0)
-        make_identity(nc, ident[:], nomemset=True)
+        nc.gpsimd.memset(ks[:].bitcast(I32), 0)
         nc.vector.memset(vs_pool[:VS_ROW, VS_SPLIT:], 0.0)
         nc.gpsimd.memset(vs_pool[:VS_ROW, :VS_SPLIT], 0.0)
-        nc.gpsimd.memset(ks[:].bitcast(I32), 0)
+        nc.gpsimd.memset(ident[:], 0.0)
+        make_identity(nc, ident[:], nomemset=True)
         nc.gpsimd.memset(vsc_words[:SCALE_ROW0, :], 0)
         nc.gpsimd.memset(vsc[:].bitcast(I32), 0)
 
@@ -71,7 +71,6 @@ def tile_attend_pkv8_rel2_gate_kernel(
             in_=v_scales.rearrange("u f e -> f u e").bitcast(I32),
         )
         nc.sync.dma_start(out=kw_pool[:], in_=k_words[0].rearrange("p t r -> p (t r)").bitcast(I32))
-        nc.sync.dma_start(out=og_raw[:], in_=og[0].rearrange("(h p) e -> p h e", p=P))
 
         def place_scale_rows(plane, gathered):
             for quad in range(QUADS):
@@ -84,11 +83,13 @@ def tile_attend_pkv8_rel2_gate_kernel(
         ks_rows = keep.tile([P, N], U8, name="ks_rows", align_bytes=64)
         nc.vector.tensor_copy(ks_rows[:], ks_pool[:, :T].indirect(key_list[:]))
         place_scale_rows(ks, ks_rows)
-        vw_pool = keep.tile([P, POOL_PAGES * DV], I32, name="vw_pool", tag="ks_pool", align_bytes=64)
+        vw_pool = shared.tile([P, POOL_PAGES * DV], I32, name="vw_pool", align_bytes=64, offset=1024)
+        og_raw = shared.tile([P, BLOCKS, DV], F32, name="og_raw", align_bytes=64, offset=0)
         nc.sync.dma_start(
             out=vw_pool[:].rearrange("p (u e) -> p u e", u=POOL_PAGES),
             in_=v_words.rearrange("u p e r -> p u (e r)").bitcast(I32),
         )
+        nc.sync.dma_start(out=og_raw[:], in_=og[0].rearrange("(h p) e -> p h e", p=P))
         vs_row = keep.tile([P, N], F32, name="vs_row")
         for g in range(PAGES):
             nc.vector.tensor_copy(
@@ -112,8 +113,12 @@ def tile_attend_pkv8_rel2_gate_kernel(
         vs_col = keep.tile([P, PAGES, PACK], F32, name="vs_col")
         for g in range(PAGES):
             vs_turned = psum.tile([P, PACK, P], F32, name="vs_turned", tag="turn%d" % (BLOCKS + g))
+            vs_dealt = keep.tile([P, PACK, P], F32, name="vs_dealt%d" % g)
+            nc.scalar.activation(
+                vs_dealt[:], vs_row[:, g * PAGE : (g + 1) * PAGE].rearrange("p (s r) -> p r s", r=PACK), ACT.Copy
+            )
             for r in range(PACK):
-                nc.tensor.transpose(vs_turned[:, r, :], vs_row[:, g * PAGE + r : (g + 1) * PAGE : PACK], ident[:])
+                nc.tensor.transpose(vs_turned[:, r, :], vs_dealt[:, r, :], ident[:])
             nc.scalar.activation(vs_col[:, g, :], vs_turned[:, :, VS_ROW], ACT.Copy)
 
         kw = keep.tile([P, N], U32, name="kw", align_bytes=64)
@@ -123,24 +128,19 @@ def tile_attend_pkv8_rel2_gate_kernel(
                 kw_pool[:].bitcast(U32).indirect(key_list[:, g * PAGE_COLS : (g + 1) * PAGE_COLS]),
             )
 
-        gate = keep.tile([P, BLOCKS, DV], F32, name="gate")
-        og_tanh = keep.tile([P, BLOCKS, DV], F32, name="og_tanh")
-        nc.scalar.activation(og_tanh[:], og_raw[:], ACT.Tanh, scale=0.5)
-        nc.scalar.activation(gate[:], og_tanh[:], ACT.Copy, scale=0.5, bias=0.5)
-
         vw = keep.tile([P, PAGES * DV], U32, name="vw", align_bytes=64)
         nc.vector.tensor_copy(vw[:], vw_pool[:].bitcast(U32).indirect(val_list[:]))
 
         sums = keep.tile([P, BLOCKS, PAGES], F32, name="sums")
         pos = [
-            keep.tile([P, BLOCKS, PACK, P], F32, name="pos", tag=tag, align_bytes=64)
-            for tag in ("pos_first", "ks_pool")
+            keep.tile([P, BLOCKS, PACK, P], F32, name="pos_first", align_bytes=64),
+            shared.tile([P, BLOCKS, PACK, P], F32, name="pos_last", align_bytes=64, offset=1024),
         ]
         w_bf = [
             keep.tile([P, NQ, PACK], BF16, name="w_bf", tag=tag, align_bytes=64) for tag in ("vsc_pool", "w_last")
         ]
 
-        def weigh(g, h):
+        def score_step(g, h):
             step = g * BLOCKS + h
             score = psum.tile([P, PAGE], F32, name="score", tag="score%d" % step)
             nc.tensor.matmul_mx(
@@ -152,6 +152,13 @@ def tile_attend_pkv8_rel2_gate_kernel(
                 start=True,
                 stop=True,
             )
+            return score
+
+        scores = [score_step(g, h) for g in range(PAGES) for h in range(BLOCKS)]
+
+        def weigh(g, h):
+            step = g * BLOCKS + h
+            score = scores[step]
             dealt = score[:].rearrange("q (s r) -> q r s", r=PACK)
             if g == 0:
                 nc.scalar.activation(pos[g][:, h], dealt, ACT.Relu)
@@ -184,6 +191,11 @@ def tile_attend_pkv8_rel2_gate_kernel(
         first_codes, first_scales = quantise(0, 0, NQ, "codes_first")
         for h in range(BLOCKS):
             weigh(1, h)
+
+        gate = keep.tile([P, BLOCKS, DV], F32, name="gate")
+        og_tanh = keep.tile([P, BLOCKS, DV], F32, name="og_tanh")
+        nc.scalar.activation(og_tanh[:], og_raw[:], ACT.Tanh, scale=0.5)
+        nc.scalar.activation(gate[:], og_tanh[:], ACT.Copy, scale=0.5, bias=0.5)
 
         for h, tag in enumerate(("weight%d" % (PAGES * BLOCKS - 1), "codes_last")):
             last_codes, last_scales = quantise(1, h * P, P, tag)

@@ -45,7 +45,7 @@ def tile_attend_pkv8_rel2_gate_kernel(
         ks_pool = shared.tile([P, T + 4], U8, name="ks_pool", align_bytes=64, offset=0)
         vsc_pool = keep.tile([P, POOL_PAGES * DV], U8, name="vsc_pool", tag="vsc_pool", align_bytes=64)
         vs_pool = keep.tile([P, T + 1], F32, name="vs_pool", align_bytes=64)
-        q_raw = keep.tile([P, PACK, NQ], F32, name="q_raw")
+        q_raw = keep.tile([P, PACK, NQ], F32, name="q_raw", tag="q_raw")
         ident = keep.tile([P, P], F32, name="ident")
 
         ks_words = ks_pool[:].bitcast(I32)
@@ -110,15 +110,17 @@ def tile_attend_pkv8_rel2_gate_kernel(
         vsc_rows = keep.tile([P, PAGES * DV], U8, name="vsc_rows", align_bytes=64)
         nc.vector.tensor_copy(vsc_rows[:], vsc_pool[:].indirect(val_list[:]))
         place_scale_rows(vsc, vsc_rows)
+        vs_dealt = keep.tile([P, PAGES, PACK, P], F32, name="vs_dealt", tag="q_raw")
         vs_col = keep.tile([P, PAGES, PACK], F32, name="vs_col")
         for g in range(PAGES):
             vs_turned = psum.tile([P, PACK, P], F32, name="vs_turned", tag="turn%d" % (BLOCKS + g))
-            vs_dealt = keep.tile([P, PACK, P], F32, name="vs_dealt%d" % g)
             nc.scalar.activation(
-                vs_dealt[:], vs_row[:, g * PAGE : (g + 1) * PAGE].rearrange("p (s r) -> p r s", r=PACK), ACT.Copy
+                vs_dealt[:, g].rearrange("p r s -> p s r"),
+                vs_row[:, g * PAGE : (g + 1) * PAGE].rearrange("p (s r) -> p s r", r=PACK),
+                ACT.Copy,
             )
             for r in range(PACK):
-                nc.tensor.transpose(vs_turned[:, r, :], vs_dealt[:, r, :], ident[:])
+                nc.tensor.transpose(vs_turned[:, r, :], vs_dealt[:, g, r, :], ident[:])
             nc.scalar.activation(vs_col[:, g, :], vs_turned[:, :, VS_ROW], ACT.Copy)
 
         kw = keep.tile([P, N], U32, name="kw", align_bytes=64)

@@ -24,6 +24,7 @@ BLOCKS = NQ // P
 PAGE_COLS = PAGE // 16
 SCALE_ROWS = 16
 SCALE_ROW0 = P - SCALE_ROWS
+KS_ROW0 = 48
 VS_ROW = P - 1
 VS_SPLIT = 3200
 
@@ -52,17 +53,18 @@ def tile_attend_pkv8_rel2_gate_kernel(
         vsc_words = vsc_pool[:].bitcast(I32)
         ks = keep.tile([P, N], U8, name="ks", align_bytes=64)
         vsc = keep.tile([P, PAGES * DV], U8, name="vsc", align_bytes=64)
-        nc.vector.memset(ks_words[:SCALE_ROW0, :], 0)
+        nc.vector.memset(ks_words[:KS_ROW0, :], 0)
+        nc.gpsimd.memset(ks_words[KS_ROW0 + SCALE_ROWS :, :], 0)
         nc.gpsimd.memset(ks[:].bitcast(I32), 0)
+        nc.gpsimd.memset(vsc_words[:SCALE_ROW0, :], 0)
         nc.vector.memset(vs_pool[:VS_ROW, VS_SPLIT:], 0.0)
         nc.gpsimd.memset(vs_pool[:VS_ROW, :VS_SPLIT], 0.0)
         nc.gpsimd.memset(ident[:], 0.0)
         make_identity(nc, ident[:], nomemset=True)
-        nc.gpsimd.memset(vsc_words[:SCALE_ROW0, :], 0)
         nc.gpsimd.memset(vsc[:].bitcast(I32), 0)
 
         nc.sync.dma_start(key_list[:], offs)
-        nc.sync.dma_start(out=ks_words[SCALE_ROW0:, : T // 4], in_=k_scales[0].bitcast(I32))
+        nc.sync.dma_start(out=ks_words[KS_ROW0 : KS_ROW0 + SCALE_ROWS, : T // 4], in_=k_scales[0].bitcast(I32))
         nc.sync.dma_start(out=vs_pool[VS_ROW:, :T], in_=vs[0:1, :])
         nc.sync.dma_start(out=q_raw[:], in_=qT[0].rearrange("(p r) q -> p r q", r=PACK))
         nc.sync.dma_start(val_list[:], voffs)
@@ -72,9 +74,9 @@ def tile_attend_pkv8_rel2_gate_kernel(
         )
         nc.sync.dma_start(out=kw_pool[:], in_=k_words[0].rearrange("p t r -> p (t r)").bitcast(I32))
 
-        def place_scale_rows(plane, gathered):
+        def place_scale_rows(plane, gathered, row0):
             for quad in range(QUADS):
-                first = SCALE_ROW0 + 4 * quad
+                first = row0 + 4 * quad
                 nc.sync.dma_start(
                     out=plane[32 * quad : 32 * quad + 4, :].bitcast(I32),
                     in_=gathered[first : first + 4, :].bitcast(I32),
@@ -82,7 +84,7 @@ def tile_attend_pkv8_rel2_gate_kernel(
 
         ks_rows = keep.tile([P, N], U8, name="ks_rows", align_bytes=64)
         nc.vector.tensor_copy(ks_rows[:], ks_pool[:, :T].indirect(key_list[:]))
-        place_scale_rows(ks, ks_rows)
+        place_scale_rows(ks, ks_rows, KS_ROW0)
         vw_pool = shared.tile([P, POOL_PAGES * DV], I32, name="vw_pool", align_bytes=64, offset=1024)
         og_raw = shared.tile([P, BLOCKS, DV], F32, name="og_raw", align_bytes=64, offset=0)
         nc.sync.dma_start(
@@ -90,12 +92,9 @@ def tile_attend_pkv8_rel2_gate_kernel(
             in_=v_words.rearrange("u p e r -> p u (e r)").bitcast(I32),
         )
         nc.sync.dma_start(out=og_raw[:], in_=og[0].rearrange("(h p) e -> p h e", p=P))
-        vs_row = keep.tile([P, N], F32, name="vs_row")
-        for g in range(PAGES):
-            nc.vector.tensor_copy(
-                vs_row[:, g * PAGE : (g + 1) * PAGE],
-                vs_pool[:, :T].indirect(key_list[:, g * PAGE_COLS : (g + 1) * PAGE_COLS]),
-            )
+        vsc_rows = keep.tile([P, PAGES * DV], U8, name="vsc_rows", align_bytes=64)
+        nc.vector.tensor_copy(vsc_rows[:], vsc_pool[:].indirect(val_list[:]))
+        place_scale_rows(vsc, vsc_rows, SCALE_ROW0)
         q_bf = keep.tile([P, NQ, PACK], BF16, name="q_bf", align_bytes=64)
         q_codes = keep.tile([P, NQ], U32, name="q_codes", align_bytes=64)
         q_scales = keep.tile([P, NQ], U8, name="q_scales", align_bytes=64)
@@ -107,21 +106,14 @@ def tile_attend_pkv8_rel2_gate_kernel(
         nc.vector.quantize_mx(
             out=q_codes[:].bitcast(FP8X4), scales=q_scales[:], in_=q_bf[:].rearrange("p q r -> p (q r)")
         )
-        vsc_rows = keep.tile([P, PAGES * DV], U8, name="vsc_rows", align_bytes=64)
-        nc.vector.tensor_copy(vsc_rows[:], vsc_pool[:].indirect(val_list[:]))
-        place_scale_rows(vsc, vsc_rows)
-        vs_dealt = keep.tile([P, PAGES, PACK, P], F32, name="vs_dealt", tag="q_raw")
-        vs_col = keep.tile([P, PAGES, PACK], F32, name="vs_col")
+        vs_row = keep.tile([P, N], F32, name="vs_row", tag="q_raw")
+        vs_col = [keep.tile([P, PACK], F32, name="vs_col", tag="vs_col%d" % g) for g in range(PAGES)]
         for g in range(PAGES):
-            vs_turned = psum.tile([P, PACK, P], F32, name="vs_turned", tag="turn%d" % (BLOCKS + g))
-            nc.scalar.activation(
-                vs_dealt[:, g].rearrange("p r s -> p s r"),
-                vs_row[:, g * PAGE : (g + 1) * PAGE].rearrange("p (s r) -> p s r", r=PACK),
-                ACT.Copy,
+            nc.vector.tensor_copy(
+                vs_row[:, g * PAGE : (g + 1) * PAGE],
+                vs_pool[:, :T].indirect(key_list[:, g * PAGE_COLS : (g + 1) * PAGE_COLS]),
             )
-            for r in range(PACK):
-                nc.tensor.transpose(vs_turned[:, r, :], vs_dealt[:, g, r, :], ident[:])
-            nc.scalar.activation(vs_col[:, g, :], vs_turned[:, :, VS_ROW], ACT.Copy)
+            nc.sync.dma_start(out=vs_col[g][:], in_=vs_row[VS_ROW:, g * PAGE : (g + 1) * PAGE])
 
         kw = keep.tile([P, N], U32, name="kw", align_bytes=64)
         for g in range(PAGES):
@@ -174,7 +166,7 @@ def tile_attend_pkv8_rel2_gate_kernel(
             nc.vector.tensor_tensor(
                 w_bf[g][:, h * P : (h + 1) * P, :],
                 turned[:].rearrange("s r q -> s q r"),
-                vs_col[:, g, :].unsqueeze(1).to_broadcast([P, P, PACK]),
+                vs_col[g][:].unsqueeze(1).to_broadcast([P, P, PACK]),
                 ALU.mult,
             )
 
@@ -203,7 +195,7 @@ def tile_attend_pkv8_rel2_gate_kernel(
             last_codes, last_scales = quantise(1, h * P, P, tag)
             total = keep.tile([P, 1], F32, name="total%d" % h)
             nc.gpsimd.tensor_scalar(total[:], sums[:, h, 0:1], sums[:, h, 1:2], 1.0, ALU.add, ALU.add)
-            inverse = keep.tile([P, 1], F32, name="inverse%d" % h)
+            inverse = keep.tile([P, 1], F32, name="inverse", tag="vs_col%d" % h)
             nc.vector.reciprocal(inverse[:], total[:])
             acc = psum.tile([P, DV], F32, name="acc", tag="turn%d" % (BLOCKS + h))
             operands = [
@@ -220,6 +212,6 @@ def tile_attend_pkv8_rel2_gate_kernel(
                     start=(g == 0),
                     stop=(g == PAGES - 1),
                 )
-            result = keep.tile([P, DV], F32, name="result%d" % h)
+            result = keep.tile([P, DV], F32, name="result", tag=("w_last", "result_last")[h], align_bytes=64)
             nc.vector.scalar_tensor_tensor(result[:], acc[:], inverse[:], gate[:, h, :], ALU.mult, ALU.mult)
             nc.sync.dma_start(out=out[0, h * P : (h + 1) * P, :], in_=result[:])

@@ -56,9 +56,9 @@ def tile_attend_pkv8_rel2_gate_kernel(
         nc.vector.memset(ks_words[:KS_ROW0, :], 0)
         nc.gpsimd.memset(ks_words[KS_ROW0 + SCALE_ROWS :, :], 0)
         nc.gpsimd.memset(ks[:].bitcast(I32), 0)
-        nc.gpsimd.memset(vsc_words[:SCALE_ROW0, :], 0)
         nc.vector.memset(vs_pool[:VS_ROW, VS_SPLIT:], 0.0)
         nc.gpsimd.memset(vs_pool[:VS_ROW, :VS_SPLIT], 0.0)
+        nc.gpsimd.memset(vsc_words[:SCALE_ROW0, :], 0)
         nc.gpsimd.memset(ident[:], 0.0)
         make_identity(nc, ident[:], nomemset=True)
         nc.gpsimd.memset(vsc[:].bitcast(I32), 0)
@@ -67,12 +67,12 @@ def tile_attend_pkv8_rel2_gate_kernel(
         nc.sync.dma_start(out=ks_words[KS_ROW0 : KS_ROW0 + SCALE_ROWS, : T // 4], in_=k_scales[0].bitcast(I32))
         nc.sync.dma_start(out=vs_pool[VS_ROW:, :T], in_=vs[0:1, :])
         nc.sync.dma_start(out=q_raw[:], in_=qT[0].rearrange("(p r) q -> p r q", r=PACK))
+        nc.sync.dma_start(out=kw_pool[:], in_=k_words[0].rearrange("p t r -> p (t r)").bitcast(I32))
         nc.sync.dma_start(val_list[:], voffs)
         nc.sync.dma_start(
             out=vsc_words[SCALE_ROW0:, :].rearrange("f (u e) -> f u e", u=POOL_PAGES),
             in_=v_scales.rearrange("u f e -> f u e").bitcast(I32),
         )
-        nc.sync.dma_start(out=kw_pool[:], in_=k_words[0].rearrange("p t r -> p (t r)").bitcast(I32))
 
         def place_scale_rows(plane, gathered, row0):
             for quad in range(QUADS):
@@ -92,9 +92,6 @@ def tile_attend_pkv8_rel2_gate_kernel(
             in_=v_words.rearrange("u p e r -> p u (e r)").bitcast(I32),
         )
         nc.sync.dma_start(out=og_raw[:], in_=og[0].rearrange("(h p) e -> p h e", p=P))
-        vsc_rows = keep.tile([P, PAGES * DV], U8, name="vsc_rows", align_bytes=64)
-        nc.vector.tensor_copy(vsc_rows[:], vsc_pool[:].indirect(val_list[:]))
-        place_scale_rows(vsc, vsc_rows, SCALE_ROW0)
         q_bf = keep.tile([P, NQ, PACK], BF16, name="q_bf", align_bytes=64)
         q_codes = keep.tile([P, NQ], U32, name="q_codes", align_bytes=64)
         q_scales = keep.tile([P, NQ], U8, name="q_scales", align_bytes=64)
@@ -122,6 +119,9 @@ def tile_attend_pkv8_rel2_gate_kernel(
                 kw_pool[:].bitcast(U32).indirect(key_list[:, g * PAGE_COLS : (g + 1) * PAGE_COLS]),
             )
 
+        vsc_rows = keep.tile([P, PAGES * DV], U8, name="vsc_rows", align_bytes=64)
+        nc.vector.tensor_copy(vsc_rows[:], vsc_pool[:].indirect(val_list[:]))
+        place_scale_rows(vsc, vsc_rows, SCALE_ROW0)
         vw = keep.tile([P, PAGES * DV], U32, name="vw", align_bytes=64)
         nc.vector.tensor_copy(vw[:], vw_pool[:].bitcast(U32).indirect(val_list[:]))
 

@@ -26,7 +26,7 @@ SCALE_ROWS = 16
 SCALE_ROW0 = P - SCALE_ROWS
 KS_ROW0 = 48
 VS_ROW = P - 1
-VS_SPLIT = 3200
+VS_SPLIT = 2944
 
 FLOPS = 2 * NQ * N * D + 2 * NQ * N * DV
 

@@ -122,16 +122,9 @@ def tile_attend_pkv8_rel2_gate_kernel(
         vsc_rows = keep.tile([P, PAGES * DV], U8, name="vsc_rows", align_bytes=64)
         nc.vector.tensor_copy(vsc_rows[:], vsc_pool[:].indirect(val_list[:]))
         place_scale_rows(vsc, vsc_rows, SCALE_ROW0)
-        vw = keep.tile([P, PAGES * DV], U32, name="vw", align_bytes=64)
-        nc.vector.tensor_copy(vw[:], vw_pool[:].bitcast(U32).indirect(val_list[:]))
-
         sums = keep.tile([P, BLOCKS, PAGES], F32, name="sums")
-        pos = [
-            keep.tile([P, BLOCKS, PACK, P], F32, name="pos_first", align_bytes=64),
-            shared.tile([P, BLOCKS, PACK, P], F32, name="pos_last", align_bytes=64, offset=1024),
-        ]
         w_bf = [
-            keep.tile([P, NQ, PACK], BF16, name="w_bf", tag=tag, align_bytes=64) for tag in ("vsc_pool", "w_last")
+            keep.tile([P, NQ, PACK], BF16, name="w_bf", tag=tag, align_bytes=64) for tag in ("w_first", "w_last")
         ]
 
         def score_step(g, h):
@@ -154,12 +147,14 @@ def tile_attend_pkv8_rel2_gate_kernel(
             step = g * BLOCKS + h
             score = scores[step]
             dealt = score[:].rearrange("q (s r) -> q r s", r=PACK)
+            tag = ("pos0", "pos1", "vsc_pool", "pos3")[step]
+            pos = keep.tile([P, PACK, P], F32, name="pos", tag=tag, align_bytes=64)
             if g == 0:
-                nc.scalar.activation(pos[g][:, h], dealt, ACT.Relu)
+                nc.scalar.activation(pos[:], dealt, ACT.Relu)
             else:
-                nc.vector.tensor_scalar(pos[g][:, h], dealt, 0.0, None, ALU.max)
+                nc.vector.tensor_scalar(pos[:], dealt, 0.0, None, ALU.max)
             weight = keep.tile([P, PACK, P], F32, name="weight", tag="weight%d" % step, align_bytes=64)
-            nc.scalar.activation(weight[:], pos[g][:, h], ACT.Square, accum_out=sums[:, h, g : g + 1])
+            nc.scalar.activation(weight[:], pos[:], ACT.Square, accum_out=sums[:, h, g : g + 1])
             turned = psum.tile([P, PACK, P], F32, name="turned", tag="turn%d" % step)
             for r in range(PACK):
                 nc.tensor.transpose(turned[:, r, :], weight[:, r, :], ident[:])
@@ -185,6 +180,9 @@ def tile_attend_pkv8_rel2_gate_kernel(
         first_codes, first_scales = quantise(0, 0, NQ, "codes_first")
         for h in range(BLOCKS):
             weigh(1, h)
+
+        vw = keep.tile([P, PAGES * DV], U32, name="vw", tag="pos0", align_bytes=64)
+        nc.vector.tensor_copy(vw[:], vw_pool[:].bitcast(U32).indirect(val_list[:]))
 
         gate = keep.tile([P, BLOCKS, DV], F32, name="gate")
         og_tanh = keep.tile([P, BLOCKS, DV], F32, name="og_tanh")

@@ -112,6 +112,18 @@ def tile_attend_pkv8_rel2_gate_kernel(
             )
             nc.sync.dma_start(out=vs_col[g][:], in_=vs_row[VS_ROW:, g * PAGE : (g + 1) * PAGE])
 
+        warm = psum.tile([P, 2, NQ], F32, name="warm", tag="turn0")
+        for half in range(2):
+            nc.tensor.matmul_mx(
+                out=warm[:, half, :],
+                lhsT=kw_pool[:, :P].bitcast(FP8X4),
+                lhsT_scale=q_scales[:, :P],
+                rhs=q_codes[:].bitcast(FP8X4),
+                rhs_scale=q_scales[:],
+                start=True,
+                stop=True,
+            )
+
         kw = keep.tile([P, N], U32, name="kw", align_bytes=64)
         for g in range(PAGES):
             nc.vector.tensor_copy(
@@ -122,7 +134,8 @@ def tile_attend_pkv8_rel2_gate_kernel(
         vsc_rows = keep.tile([P, PAGES * DV], U8, name="vsc_rows", align_bytes=64)
         nc.vector.tensor_copy(vsc_rows[:], vsc_pool[:].indirect(val_list[:]))
         place_scale_rows(vsc, vsc_rows, SCALE_ROW0)
-        sums = keep.tile([P, BLOCKS, PAGES], F32, name="sums")
+        sums = keep.tile([P, BLOCKS, 5], F32, name="sums")
+        nc.gpsimd.memset(sums[:, :, 4:5], 1.0)
         w_bf = [
             keep.tile([P, NQ, PACK], BF16, name="w_bf", tag=tag, align_bytes=64) for tag in ("w_first", "w_last")
         ]
@@ -141,23 +154,45 @@ def tile_attend_pkv8_rel2_gate_kernel(
             )
             return score
 
-        scores = [score_step(g, h) for g in range(PAGES) for h in range(BLOCKS)]
+        scores = [score_step(0, 0), score_step(0, 1), score_step(1, 0)]
 
-        def weigh(g, h):
-            step = g * BLOCKS + h
-            score = scores[step]
-            dealt = score[:].rearrange("q (s r) -> q r s", r=PACK)
-            tag = ("pos0", "pos1", "vsc_pool", "pos3")[step]
-            pos = keep.tile([P, PACK, P], F32, name="pos", tag=tag, align_bytes=64)
-            if g == 0:
-                nc.scalar.activation(pos[:], dealt, ACT.Relu)
+        pos = {}
+        weight = {}
+
+        def rectify(step, on_vector=False):
+            pos[step] = keep.tile([P, PACK, P], F32, name="pos", tag="pos%d" % step, align_bytes=64)
+            weight[step] = [
+                keep.tile([P, 2, P], F32, name="weight", tag="weight%d%s" % (step, "ab"[half]), align_bytes=64)
+                for half in range(2)
+            ]
+            dealt = scores[step][:].rearrange("q (s r) -> q r s", r=PACK)
+            if on_vector:
+                nc.vector.tensor_scalar(pos[step][:], dealt, 0.0, None, ALU.max)
+            elif step in (0, 3):
+                for rows in (slice(0, 2), slice(2, 4)):
+                    nc.scalar.activation(pos[step][:, rows], dealt[:, rows], ACT.Relu)
             else:
-                nc.vector.tensor_scalar(pos[:], dealt, 0.0, None, ALU.max)
-            weight = keep.tile([P, PACK, P], F32, name="weight", tag="weight%d" % step, align_bytes=64)
-            nc.scalar.activation(weight[:], pos[:], ACT.Square, accum_out=sums[:, h, g : g + 1])
+                nc.scalar.activation(pos[step][:], dealt, ACT.Relu)
+
+        def square(step, rows, part):
+            g, h = divmod(step, BLOCKS)
+            nc.scalar.activation(
+                weight[step][rows.start // 2][:], pos[step][:, rows], ACT.Square, accum_out=sums[:, h, part : part + 1]
+            )
+
+        def square_gpsimd(step, rows):
+            nc.gpsimd.tensor_tensor(weight[step][rows.start // 2][:], pos[step][:, rows], pos[step][:, rows], ALU.mult)
+
+        def sum_late(step, rows, part):
+            g, h = divmod(step, BLOCKS)
+            spare = keep.tile([P, 2, P], F32, name="spare", tag="pos3", align_bytes=64)
+            nc.scalar.activation(spare[:], weight[step][rows.start // 2][:], ACT.Copy, accum_out=sums[:, h, part : part + 1])
+
+        def turn(step):
+            g, h = divmod(step, BLOCKS)
             turned = psum.tile([P, PACK, P], F32, name="turned", tag="turn%d" % step)
             for r in range(PACK):
-                nc.tensor.transpose(turned[:, r, :], weight[:, r, :], ident[:])
+                nc.tensor.transpose(turned[:, r, :], weight[step][r // 2][:, r % 2, :], ident[:])
             nc.vector.tensor_tensor(
                 w_bf[g][:, h * P : (h + 1) * P, :],
                 turned[:].rearrange("s r q -> s q r"),
@@ -175,26 +210,46 @@ def tile_attend_pkv8_rel2_gate_kernel(
             )
             return codes, scales
 
-        for h in range(BLOCKS):
-            weigh(0, h)
-        first_codes, first_scales = quantise(0, 0, NQ, "codes_first")
-        for h in range(BLOCKS):
-            weigh(1, h)
-
+        low, high = slice(0, 2), slice(2, 4)
+        rectify(0)
+        square(0, low, 0)
+        square(0, high, 3)
+        rectify(1, on_vector=True)
         vw = keep.tile([P, PAGES * DV], U32, name="vw", tag="pos0", align_bytes=64)
         nc.vector.tensor_copy(vw[:], vw_pool[:].bitcast(U32).indirect(val_list[:]))
+        turn(0)
+        scores.append(score_step(1, 1))
+        rectify(2)
+        square_gpsimd(1, high)
+        square(1, low, 0)
+        square_gpsimd(2, high)
+        square(2, low, 1)
+        rectify(3)
+        square(3, low, 1)
+        square(3, high, 2)
+        turn(1)
+        turn(2)
+        turn(3)
+        first_codes, first_scales = quantise(0, 0, NQ, "weight3a")
+        sum_late(2, high, 2)
+        sum_late(1, high, 3)
+
+        totals = []
+        for h in range(BLOCKS):
+            total = keep.tile([P, 1], F32, name="total%d" % h)
+            terms = keep.tile([P, 5], F32, name="terms%d" % h)
+            nc.scalar.activation(terms[:], sums[:, h, :], ACT.Copy, accum_out=total[:])
+            totals.append(total)
 
         gate = keep.tile([P, BLOCKS, DV], F32, name="gate")
         og_tanh = keep.tile([P, BLOCKS, DV], F32, name="og_tanh")
         nc.scalar.activation(og_tanh[:], og_raw[:], ACT.Tanh, scale=0.5)
         nc.scalar.activation(gate[:], og_tanh[:], ACT.Copy, scale=0.5, bias=0.5)
 
-        for h, tag in enumerate(("weight%d" % (PAGES * BLOCKS - 1), "codes_last")):
+        for h, tag in enumerate(("weight3b", "codes_last")):
             last_codes, last_scales = quantise(1, h * P, P, tag)
-            total = keep.tile([P, 1], F32, name="total%d" % h)
-            nc.gpsimd.tensor_scalar(total[:], sums[:, h, 0:1], sums[:, h, 1:2], 1.0, ALU.add, ALU.add)
             inverse = keep.tile([P, 1], F32, name="inverse", tag="vs_col%d" % h)
-            nc.vector.reciprocal(inverse[:], total[:])
+            nc.vector.reciprocal(inverse[:], totals[h][:])
             acc = psum.tile([P, DV], F32, name="acc", tag="turn%d" % (BLOCKS + h))
             operands = [
                 (first_codes[:, h * P : (h + 1) * P], first_scales[:, h * P : (h + 1) * P]),

@@ -51,17 +51,13 @@ def tile_attend_pkv8_rel2_gate_kernel(
 
         ks_words = ks_pool[:].bitcast(I32)
         vsc_words = vsc_pool[:].bitcast(I32)
-        ks = keep.tile([P, N], U8, name="ks", align_bytes=64)
-        vsc = keep.tile([P, PAGES * DV], U8, name="vsc", align_bytes=64)
+        nc.gpsimd.memset(ident[:], 0.0)
+        make_identity(nc, ident[:], nomemset=True)
         nc.vector.memset(ks_words[:KS_ROW0, :], 0)
         nc.gpsimd.memset(ks_words[KS_ROW0 + SCALE_ROWS :, :], 0)
-        nc.gpsimd.memset(ks[:].bitcast(I32), 0)
         nc.vector.memset(vs_pool[:VS_ROW, VS_SPLIT:], 0.0)
         nc.gpsimd.memset(vs_pool[:VS_ROW, :VS_SPLIT], 0.0)
         nc.gpsimd.memset(vsc_words[:SCALE_ROW0, :], 0)
-        nc.gpsimd.memset(ident[:], 0.0)
-        make_identity(nc, ident[:], nomemset=True)
-        nc.gpsimd.memset(vsc[:].bitcast(I32), 0)
 
         nc.sync.dma_start(key_list[:], offs)
         nc.sync.dma_start(out=ks_words[KS_ROW0 : KS_ROW0 + SCALE_ROWS, : T // 4], in_=k_scales[0].bitcast(I32))
@@ -84,8 +80,9 @@ def tile_attend_pkv8_rel2_gate_kernel(
 
         ks_rows = keep.tile([P, N], U8, name="ks_rows", align_bytes=64)
         nc.vector.tensor_copy(ks_rows[:], ks_pool[:, :T].indirect(key_list[:]))
+        ks = shared.tile([P, N], U8, name="ks", align_bytes=64, offset=1024)
         place_scale_rows(ks, ks_rows, KS_ROW0)
-        vw_pool = shared.tile([P, POOL_PAGES * DV], I32, name="vw_pool", align_bytes=64, offset=1024)
+        vw_pool = shared.tile([P, POOL_PAGES * DV], I32, name="vw_pool", align_bytes=64, offset=2048)
         og_raw = shared.tile([P, BLOCKS, DV], F32, name="og_raw", align_bytes=64, offset=0)
         nc.sync.dma_start(
             out=vw_pool[:].rearrange("p (u e) -> p u e", u=POOL_PAGES),
@@ -133,6 +130,7 @@ def tile_attend_pkv8_rel2_gate_kernel(
 
         vsc_rows = keep.tile([P, PAGES * DV], U8, name="vsc_rows", align_bytes=64)
         nc.vector.tensor_copy(vsc_rows[:], vsc_pool[:].indirect(val_list[:]))
+        vsc = keep.tile([P, PAGES * DV], U8, name="vsc", tag="vsc_pool", align_bytes=64)
         place_scale_rows(vsc, vsc_rows, SCALE_ROW0)
         sums = keep.tile([P, BLOCKS, 5], F32, name="sums")
         nc.gpsimd.memset(sums[:, :, 4:5], 1.0)

@@ -109,18 +109,6 @@ def tile_attend_pkv8_rel2_gate_kernel(
             )
             nc.sync.dma_start(out=vs_col[g][:], in_=vs_row[VS_ROW:, g * PAGE : (g + 1) * PAGE])
 
-        warm = psum.tile([P, 2, NQ], F32, name="warm", tag="turn0")
-        for half in range(2):
-            nc.tensor.matmul_mx(
-                out=warm[:, half, :],
-                lhsT=kw_pool[:, :P].bitcast(FP8X4),
-                lhsT_scale=q_scales[:, :P],
-                rhs=q_codes[:].bitcast(FP8X4),
-                rhs_scale=q_scales[:],
-                start=True,
-                stop=True,
-            )
-
         kw = keep.tile([P, N], U32, name="kw", align_bytes=64)
         for g in range(PAGES):
             nc.vector.tensor_copy(

@@ -153,7 +153,8 @@ def tile_attend_pkv8_rel2_gate_kernel(
             ]
             dealt = scores[step][:].rearrange("q (s r) -> q r s", r=PACK)
             if on_vector:
-                nc.vector.tensor_scalar(pos[step][:], dealt, 0.0, None, ALU.max)
+                for rows in (slice(2, 4), slice(0, 2)):
+                    nc.vector.tensor_scalar(pos[step][:, rows], dealt[:, rows], 0.0, None, ALU.max)
             elif step in (0, 3):
                 for rows in (slice(0, 2), slice(2, 4)):
                     nc.scalar.activation(pos[step][:, rows], dealt[:, rows], ACT.Relu)

@@ -21,9 +21,10 @@ PAGE = 512
 PAGES = N // PAGE
 POOL_PAGES = T // PAGE
 BLOCKS = NQ // P
-PAGE_COLS = PAGE // 16
+HALF = P // 2
+LIST_STEP = 16
 SCALE_ROWS = 16
-SCALE_ROW0 = P - SCALE_ROWS
+VSC_ROW0 = P - SCALE_ROWS
 KS_ROW0 = 48
 VS_ROW = P - 1
 VS_SPLIT = 2944
@@ -40,13 +41,13 @@ def tile_attend_pkv8_rel2_gate_kernel(
         shared = ctx.enter_context(tc.tile_pool(name="shared", bufs=1))
         psum = ctx.enter_context(tc.psum_pool(name="psum", bufs=1))
 
-        key_list = keep.tile([P, N // 16], U16, name="key_list")
-        val_list = keep.tile([P, PAGES * DV // 16], U16, name="val_list")
+        key_list = keep.tile([P, N // LIST_STEP], U16, name="key_list")
+        val_list = keep.tile([P, PAGES * DV // LIST_STEP], U16, name="val_list")
         kw_pool = keep.tile([P, T], I32, name="kw_pool", align_bytes=64)
         ks_pool = shared.tile([P, T + 4], U8, name="ks_pool", align_bytes=64, offset=0)
         vsc_pool = keep.tile([P, POOL_PAGES * DV], U8, name="vsc_pool", tag="vsc_pool", align_bytes=64)
         vs_pool = keep.tile([P, T + 1], F32, name="vs_pool", align_bytes=64)
-        q_raw = keep.tile([P, PACK, NQ], F32, name="q_raw", tag="q_raw")
+        q_raw = keep.tile([P, PACK, NQ], F32, name="q_raw")
         ident = keep.tile([P, P], F32, name="ident")
 
         ks_words = ks_pool[:].bitcast(I32)
@@ -55,20 +56,23 @@ def tile_attend_pkv8_rel2_gate_kernel(
         make_identity(nc, ident[:], nomemset=True)
         nc.vector.memset(ks_words[:KS_ROW0, :], 0)
         nc.gpsimd.memset(ks_words[KS_ROW0 + SCALE_ROWS :, :], 0)
+        nc.gpsimd.memset(vsc_words[:VSC_ROW0, :], 0)
         nc.vector.memset(vs_pool[:VS_ROW, VS_SPLIT:], 0.0)
         nc.gpsimd.memset(vs_pool[:VS_ROW, :VS_SPLIT], 0.0)
-        nc.gpsimd.memset(vsc_words[:SCALE_ROW0, :], 0)
 
         nc.sync.dma_start(key_list[:], offs)
         nc.sync.dma_start(out=ks_words[KS_ROW0 : KS_ROW0 + SCALE_ROWS, : T // 4], in_=k_scales[0].bitcast(I32))
         nc.sync.dma_start(out=vs_pool[VS_ROW:, :T], in_=vs[0:1, :])
         nc.sync.dma_start(out=q_raw[:], in_=qT[0].rearrange("(p r) q -> p r q", r=PACK))
-        nc.sync.dma_start(out=kw_pool[:], in_=k_words[0].rearrange("p t r -> p (t r)").bitcast(I32))
         nc.sync.dma_start(val_list[:], voffs)
         nc.sync.dma_start(
-            out=vsc_words[SCALE_ROW0:, :].rearrange("f (u e) -> f u e", u=POOL_PAGES),
+            out=vsc_words[VSC_ROW0:, :].rearrange("f (u e) -> f u e", u=POOL_PAGES),
             in_=v_scales.rearrange("u f e -> f u e").bitcast(I32),
         )
+        nc.sync.dma_start(out=kw_pool[:], in_=k_words[0].rearrange("p t r -> p (t r)").bitcast(I32))
+
+        def slots(first, count):
+            return key_list[:, first // LIST_STEP : (first + count) // LIST_STEP]
 
         def place_scale_rows(plane, gathered, row0):
             for quad in range(QUADS):
@@ -80,15 +84,21 @@ def tile_attend_pkv8_rel2_gate_kernel(
 
         ks_rows = keep.tile([P, N], U8, name="ks_rows", align_bytes=64)
         nc.vector.tensor_copy(ks_rows[:], ks_pool[:, :T].indirect(key_list[:]))
+        ks_dealt = keep.tile([P, N], U8, name="ks_dealt", align_bytes=64)
+        nc.vector.tensor_copy(
+            ks_dealt[:].rearrange("p (g r s) -> p g s r", g=PAGES, r=PACK),
+            ks_rows[:].rearrange("p (g s r) -> p g s r", g=PAGES, r=PACK),
+        )
         ks = shared.tile([P, N], U8, name="ks", align_bytes=64, offset=1024)
-        place_scale_rows(ks, ks_rows, KS_ROW0)
-        vw_pool = shared.tile([P, POOL_PAGES * DV], I32, name="vw_pool", align_bytes=64, offset=2048)
+        place_scale_rows(ks, ks_dealt, KS_ROW0)
         og_raw = shared.tile([P, BLOCKS, DV], F32, name="og_raw", align_bytes=64, offset=0)
+        vw_pool = shared.tile([P, POOL_PAGES * DV], I32, name="vw_pool", align_bytes=64, offset=2048)
         nc.sync.dma_start(
             out=vw_pool[:].rearrange("p (u e) -> p u e", u=POOL_PAGES),
             in_=v_words.rearrange("u p e r -> p u (e r)").bitcast(I32),
         )
         nc.sync.dma_start(out=og_raw[:], in_=og[0].rearrange("(h p) e -> p h e", p=P))
+
         q_bf = keep.tile([P, NQ, PACK], BF16, name="q_bf", align_bytes=64)
         q_codes = keep.tile([P, NQ], U32, name="q_codes", align_bytes=64)
         q_scales = keep.tile([P, NQ], U8, name="q_scales", align_bytes=64)
@@ -100,95 +110,84 @@ def tile_attend_pkv8_rel2_gate_kernel(
         nc.vector.quantize_mx(
             out=q_codes[:].bitcast(FP8X4), scales=q_scales[:], in_=q_bf[:].rearrange("p q r -> p (q r)")
         )
-        vs_row = keep.tile([P, N], F32, name="vs_row", tag="q_raw")
-        vs_col = [keep.tile([P, PACK], F32, name="vs_col", tag="vs_col%d" % g) for g in range(PAGES)]
-        for g in range(PAGES):
-            nc.vector.tensor_copy(
-                vs_row[:, g * PAGE : (g + 1) * PAGE],
-                vs_pool[:, :T].indirect(key_list[:, g * PAGE_COLS : (g + 1) * PAGE_COLS]),
-            )
-            nc.sync.dma_start(out=vs_col[g][:], in_=vs_row[VS_ROW:, g * PAGE : (g + 1) * PAGE])
-
-        kw = keep.tile([P, N], U32, name="kw", align_bytes=64)
-        for g in range(PAGES):
-            nc.vector.tensor_copy(
-                kw[:, g * PAGE : (g + 1) * PAGE],
-                kw_pool[:].bitcast(U32).indirect(key_list[:, g * PAGE_COLS : (g + 1) * PAGE_COLS]),
-            )
 
         vsc_rows = keep.tile([P, PAGES * DV], U8, name="vsc_rows", align_bytes=64)
         nc.vector.tensor_copy(vsc_rows[:], vsc_pool[:].indirect(val_list[:]))
         vsc = keep.tile([P, PAGES * DV], U8, name="vsc", tag="vsc_pool", align_bytes=64)
-        place_scale_rows(vsc, vsc_rows, SCALE_ROW0)
-        sums = keep.tile([P, BLOCKS, 5], F32, name="sums")
-        nc.gpsimd.memset(sums[:, :, 4:5], 1.0)
-        w_bf = [
-            keep.tile([P, NQ, PACK], BF16, name="w_bf", tag=tag, align_bytes=64) for tag in ("w_first", "w_last")
-        ]
+        place_scale_rows(vsc, vsc_rows, VSC_ROW0)
 
-        def score_step(g, h):
-            step = g * BLOCKS + h
-            score = psum.tile([P, PAGE], F32, name="score", tag="score%d" % step)
-            nc.tensor.matmul_mx(
-                out=score[:],
-                lhsT=q_codes[:, h * P : (h + 1) * P].bitcast(FP8X4),
-                lhsT_scale=q_scales[:, h * P : (h + 1) * P],
-                rhs=kw[:, g * PAGE : (g + 1) * PAGE].bitcast(FP8X4),
-                rhs_scale=ks[:, g * PAGE : (g + 1) * PAGE],
-                start=True,
-                stop=True,
-            )
-            return score
-
-        scores = [score_step(0, 0), score_step(0, 1), score_step(1, 0)]
-
-        pos = {}
-        weight = {}
-
-        def rectify(step, on_vector=False):
-            pos[step] = keep.tile([P, PACK, P], F32, name="pos", tag="pos%d" % step, align_bytes=64)
-            weight[step] = [
-                keep.tile([P, 2, P], F32, name="weight", tag="weight%d%s" % (step, "ab"[half]), align_bytes=64)
-                for half in range(2)
-            ]
-            dealt = scores[step][:].rearrange("q (s r) -> q r s", r=PACK)
-            if on_vector:
-                for rows in (slice(2, 4), slice(0, 2)):
-                    nc.vector.tensor_scalar(pos[step][:, rows], dealt[:, rows], 0.0, None, ALU.max)
-            elif step in (0, 3):
-                for rows in (slice(0, 2), slice(2, 4)):
-                    nc.scalar.activation(pos[step][:, rows], dealt[:, rows], ACT.Relu)
-            else:
-                nc.scalar.activation(pos[step][:], dealt, ACT.Relu)
-
-        def square(step, rows, part):
-            g, h = divmod(step, BLOCKS)
-            nc.scalar.activation(
-                weight[step][rows.start // 2][:], pos[step][:, rows], ACT.Square, accum_out=sums[:, h, part : part + 1]
-            )
-
-        def square_gpsimd(step, rows):
-            nc.gpsimd.tensor_tensor(weight[step][rows.start // 2][:], pos[step][:, rows], pos[step][:, rows], ALU.mult)
-
-        def sum_late(step, rows, part):
-            g, h = divmod(step, BLOCKS)
-            spare = keep.tile([P, 2, P], F32, name="spare", tag="pos3", align_bytes=64)
-            nc.scalar.activation(spare[:], weight[step][rows.start // 2][:], ACT.Copy, accum_out=sums[:, h, part : part + 1])
-
-        def turn(step):
-            g, h = divmod(step, BLOCKS)
-            turned = psum.tile([P, PACK, P], F32, name="turned", tag="turn%d" % step)
+        vs_turned = []
+        for g in range(PAGES):
+            vs_row = keep.tile([P, PAGE], F32, name="vs_row", tag="vs_row%d" % g)
+            nc.scalar.activation(vs_row[:], vs_pool[:, :T].indirect(slots(g * PAGE, PAGE)), ACT.Copy)
+            vs_turned.append(psum.tile([P, PACK, P], F32, name="vs_turned", tag="vs_turned%d" % g))
             for r in range(PACK):
-                nc.tensor.transpose(turned[:, r, :], weight[step][r // 2][:, r % 2, :], ident[:])
+                nc.tensor.transpose(vs_turned[g][:, r, :], vs_row[:, r::PACK], ident[:])
+
+        kw = [keep.tile([P, PACK, P], U32, name="kw", tag="kw%d" % g, align_bytes=64) for g in range(PAGES)]
+        for g in range(PAGES):
+            nc.vector.tensor_copy(
+                kw[g][:].rearrange("p r s -> p s r"), kw_pool[:].bitcast(U32).indirect(slots(g * PAGE, PAGE))
+            )
+
+        steps = PAGES * BLOCKS
+        scores = [psum.tile([P, PACK, P], F32, name="score", tag="score%d" % t) for t in range(steps)]
+        pos = [keep.tile([P, PACK, P], F32, name="pos", tag="pos%d" % t, align_bytes=64) for t in range(steps)]
+        weight = [keep.tile([P, PACK, P], F32, name="weight", tag="weight%d" % t, align_bytes=64) for t in range(steps)]
+        w_bf = [keep.tile([P, NQ, PACK], BF16, name="w_bf", tag="w_bf%d" % g, align_bytes=64) for g in range(PAGES)]
+        sums = [psum.tile([P, P], F32, name="sums", tag="sums%d" % h) for h in range(BLOCKS)]
+        low, high, whole = slice(0, HALF), slice(HALF, P), slice(0, P)
+
+        for t in range(steps):
+            g, h = divmod(t, BLOCKS)
+            for r in range(PACK):
+                first = g * PAGE + r * P
+                nc.tensor.matmul_mx(
+                    out=scores[t][:, r, :],
+                    lhsT=kw[g][:, r, :].bitcast(FP8X4),
+                    lhsT_scale=ks[:, first : first + P],
+                    rhs=q_codes[:, h * P : (h + 1) * P].bitcast(FP8X4),
+                    rhs_scale=q_scales[:, h * P : (h + 1) * P],
+                    start=True,
+                    stop=True,
+                )
+
+        def rectify(t, cols):
+            nc.scalar.activation(pos[t][:, :, cols], scores[t][:, :, cols], ACT.Relu)
+
+        def rectify_vector(t, cols):
+            nc.vector.tensor_scalar(pos[t][:, :, cols], scores[t][:, :, cols], 0.0, None, ALU.max)
+
+        def square(t, cols):
+            nc.scalar.activation(weight[t][:, :, cols], pos[t][:, :, cols], ACT.Square)
+
+        def square_gpsimd(t, cols):
+            nc.gpsimd.tensor_tensor(weight[t][:, :, cols], pos[t][:, :, cols], pos[t][:, :, cols], ALU.mult)
+
+        def add_up(t):
+            g, h = divmod(t, BLOCKS)
+            for r in range(PACK):
+                nc.tensor.matmul(
+                    sums[h][:],
+                    weight[t][:, r, :],
+                    ident[:],
+                    start=(g == 0 and r == 0),
+                    stop=(g == PAGES - 1 and r == PACK - 1),
+                    is_transpose=True,
+                )
+
+        def weigh(t, cols):
+            g, h = divmod(t, BLOCKS)
+            pairs = (cols.stop - cols.start) // 2
             nc.vector.tensor_tensor(
-                w_bf[g][:, h * P : (h + 1) * P, :],
-                turned[:].rearrange("s r q -> s q r"),
-                vs_col[g][:].unsqueeze(1).to_broadcast([P, P, PACK]),
+                w_bf[g][:, h * P + cols.start : h * P + cols.stop, :].rearrange("s (c i) r -> s c r i", i=2),
+                weight[t][:, :, cols].rearrange("s r (c i) -> s c r i", i=2),
+                vs_turned[g][:, :, VS_ROW:].unsqueeze(1).to_broadcast([P, pairs, PACK, 2]),
                 ALU.mult,
             )
 
         def quantise(g, first, count, tag):
-            codes = keep.tile([P, count], U32, name="w_codes", tag=tag, align_bytes=64)
+            codes = keep.tile([P, count], U32, name="w_codes", tag="codes_" + tag, align_bytes=64)
             scales = keep.tile([P, count], U8, name="w_scales", tag="scales_" + tag, align_bytes=64)
             nc.vector.quantize_mx(
                 out=codes[:].bitcast(FP8X4),
@@ -197,35 +196,37 @@ def tile_attend_pkv8_rel2_gate_kernel(
             )
             return codes, scales
 
-        low, high = slice(0, 2), slice(2, 4)
-        rectify(0)
-        square(0, low, 0)
-        square(0, high, 3)
-        rectify(1, on_vector=True)
-        vw = keep.tile([P, PAGES * DV], U32, name="vw", tag="pos0", align_bytes=64)
+        rectify(0, high)
+        rectify(0, low)
+        square_gpsimd(0, high)
+        square(0, low)
+        vw = keep.tile([P, PAGES * DV], U32, name="vw", align_bytes=64)
         nc.vector.tensor_copy(vw[:], vw_pool[:].bitcast(U32).indirect(val_list[:]))
-        turn(0)
-        scores.append(score_step(1, 1))
-        rectify(2)
+        rectify_vector(1, high)
+        rectify_vector(1, low)
         square_gpsimd(1, high)
-        square(1, low, 0)
-        square_gpsimd(2, high)
-        square(2, low, 1)
-        rectify(3)
-        square(3, low, 1)
-        square(3, high, 2)
-        turn(1)
-        turn(2)
-        turn(3)
-        first_codes, first_scales = quantise(0, 0, NQ, "weight3a")
-        sum_late(2, high, 2)
-        sum_late(1, high, 3)
+        weigh(0, whole)
+        rectify(2, low)
+        rectify(2, high)
+        square(1, low)
+        weigh(1, whole)
+        square(2, whole)
+        weigh(2, whole)
+        rectify(3, low)
+        rectify(3, high)
+        square(3, low)
+        square(3, high)
+        first_codes, first_scales = quantise(0, 0, NQ, "first")
+        weigh(3, low)
+        weigh(3, high)
+        for t in range(steps):
+            add_up(t)
 
         totals = []
         for h in range(BLOCKS):
+            spare = keep.tile([P, P], F32, name="spare", tag="spare%d" % h)
             total = keep.tile([P, 1], F32, name="total%d" % h)
-            terms = keep.tile([P, 5], F32, name="terms%d" % h)
-            nc.scalar.activation(terms[:], sums[:, h, :], ACT.Copy, accum_out=total[:])
+            nc.scalar.activation(spare[:], sums[h][:], ACT.Copy, bias=1.0 / P, accum_out=total[:])
             totals.append(total)
 
         gate = keep.tile([P, BLOCKS, DV], F32, name="gate")
@@ -233,11 +234,11 @@ def tile_attend_pkv8_rel2_gate_kernel(
         nc.scalar.activation(og_tanh[:], og_raw[:], ACT.Tanh, scale=0.5)
         nc.scalar.activation(gate[:], og_tanh[:], ACT.Copy, scale=0.5, bias=0.5)
 
-        for h, tag in enumerate(("weight3b", "codes_last")):
-            last_codes, last_scales = quantise(1, h * P, P, tag)
-            inverse = keep.tile([P, 1], F32, name="inverse", tag="vs_col%d" % h)
+        for h in range(BLOCKS):
+            last_codes, last_scales = quantise(1, h * P, P, "last%d" % h)
+            inverse = keep.tile([P, 1], F32, name="inverse", tag="w_bf%d" % h, align_bytes=64)
             nc.vector.reciprocal(inverse[:], totals[h][:])
-            acc = psum.tile([P, DV], F32, name="acc", tag="turn%d" % (BLOCKS + h))
+            acc = psum.tile([P, DV], F32, name="acc", tag="score%d" % h)
             operands = [
                 (first_codes[:, h * P : (h + 1) * P], first_scales[:, h * P : (h + 1) * P]),
                 (last_codes[:], last_scales[:]),
@@ -252,6 +253,6 @@ def tile_attend_pkv8_rel2_gate_kernel(
                     start=(g == 0),
                     stop=(g == PAGES - 1),
                 )
-            result = keep.tile([P, DV], F32, name="result", tag=("w_last", "result_last")[h], align_bytes=64)
+            result = keep.tile([P, DV], F32, name="result", tag="result%d" % h, align_bytes=64)
             nc.vector.scalar_tensor_tensor(result[:], acc[:], inverse[:], gate[:, h, :], ALU.mult, ALU.mult)
             nc.sync.dma_start(out=out[0, h * P : (h + 1) * P, :], in_=result[:])

@@ -47,29 +47,29 @@ def tile_attend_pkv8_rel2_gate_kernel(
         ks_pool = shared.tile([P, T + 4], U8, name="ks_pool", align_bytes=64, offset=0)
         vsc_pool = keep.tile([P, POOL_PAGES * DV], U8, name="vsc_pool", tag="vsc_pool", align_bytes=64)
         vs_pool = keep.tile([P, T + 1], F32, name="vs_pool", align_bytes=64)
-        q_raw = keep.tile([P, PACK, NQ], F32, name="q_raw")
+        q_raw = keep.tile([P, PACK, NQ], F32, name="q_raw", tag="q_raw")
         ident = keep.tile([P, P], F32, name="ident")
 
         ks_words = ks_pool[:].bitcast(I32)
         vsc_words = vsc_pool[:].bitcast(I32)
-        nc.gpsimd.memset(ident[:], 0.0)
-        make_identity(nc, ident[:], nomemset=True)
         nc.vector.memset(ks_words[:KS_ROW0, :], 0)
         nc.gpsimd.memset(ks_words[KS_ROW0 + SCALE_ROWS :, :], 0)
-        nc.gpsimd.memset(vsc_words[:VSC_ROW0, :], 0)
         nc.vector.memset(vs_pool[:VS_ROW, VS_SPLIT:], 0.0)
         nc.gpsimd.memset(vs_pool[:VS_ROW, :VS_SPLIT], 0.0)
+        nc.gpsimd.memset(ident[:], 0.0)
+        make_identity(nc, ident[:], nomemset=True)
+        nc.gpsimd.memset(vsc_words[:VSC_ROW0, :], 0)
 
         nc.sync.dma_start(key_list[:], offs)
         nc.sync.dma_start(out=ks_words[KS_ROW0 : KS_ROW0 + SCALE_ROWS, : T // 4], in_=k_scales[0].bitcast(I32))
         nc.sync.dma_start(out=vs_pool[VS_ROW:, :T], in_=vs[0:1, :])
         nc.sync.dma_start(out=q_raw[:], in_=qT[0].rearrange("(p r) q -> p r q", r=PACK))
+        nc.sync.dma_start(out=kw_pool[:], in_=k_words[0].rearrange("p t r -> p (t r)").bitcast(I32))
         nc.sync.dma_start(val_list[:], voffs)
         nc.sync.dma_start(
             out=vsc_words[VSC_ROW0:, :].rearrange("f (u e) -> f u e", u=POOL_PAGES),
             in_=v_scales.rearrange("u f e -> f u e").bitcast(I32),
         )
-        nc.sync.dma_start(out=kw_pool[:], in_=k_words[0].rearrange("p t r -> p (t r)").bitcast(I32))
 
         def slots(first, count):
             return key_list[:, first // LIST_STEP : (first + count) // LIST_STEP]
@@ -82,17 +82,17 @@ def tile_attend_pkv8_rel2_gate_kernel(
                     in_=gathered[first : first + 4, :].bitcast(I32),
                 )
 
-        ks_rows = keep.tile([P, N], U8, name="ks_rows", align_bytes=64)
+        ks_rows = shared.tile([P, N], U8, name="ks_rows", align_bytes=64, offset=4160)
         nc.vector.tensor_copy(ks_rows[:], ks_pool[:, :T].indirect(key_list[:]))
-        ks_dealt = keep.tile([P, N], U8, name="ks_dealt", align_bytes=64)
+        ks_dealt = keep.tile([P, N], U8, name="ks_dealt", tag="ks_dealt", align_bytes=64)
         nc.vector.tensor_copy(
             ks_dealt[:].rearrange("p (g r s) -> p g s r", g=PAGES, r=PACK),
             ks_rows[:].rearrange("p (g s r) -> p g s r", g=PAGES, r=PACK),
         )
         ks = shared.tile([P, N], U8, name="ks", align_bytes=64, offset=1024)
         place_scale_rows(ks, ks_dealt, KS_ROW0)
-        og_raw = shared.tile([P, BLOCKS, DV], F32, name="og_raw", align_bytes=64, offset=0)
-        vw_pool = shared.tile([P, POOL_PAGES * DV], I32, name="vw_pool", align_bytes=64, offset=2048)
+        og_raw = shared.tile([P, BLOCKS, DV], F32, name="og_raw", align_bytes=64, offset=3648)
+        vw_pool = shared.tile([P, POOL_PAGES * DV], I32, name="vw_pool", align_bytes=64, offset=4672)
         nc.sync.dma_start(
             out=vw_pool[:].rearrange("p (u e) -> p u e", u=POOL_PAGES),
             in_=v_words.rearrange("u p e r -> p u (e r)").bitcast(I32),
@@ -111,15 +111,11 @@ def tile_attend_pkv8_rel2_gate_kernel(
             out=q_codes[:].bitcast(FP8X4), scales=q_scales[:], in_=q_bf[:].rearrange("p q r -> p (q r)")
         )
 
-        vsc_rows = keep.tile([P, PAGES * DV], U8, name="vsc_rows", align_bytes=64)
-        nc.vector.tensor_copy(vsc_rows[:], vsc_pool[:].indirect(val_list[:]))
-        vsc = keep.tile([P, PAGES * DV], U8, name="vsc", tag="vsc_pool", align_bytes=64)
-        place_scale_rows(vsc, vsc_rows, VSC_ROW0)
-
         vs_turned = []
+        vs_rows = keep.tile([P, N], F32, name="vs_rows", tag="q_raw")
         for g in range(PAGES):
-            vs_row = keep.tile([P, PAGE], F32, name="vs_row", tag="vs_row%d" % g)
-            nc.scalar.activation(vs_row[:], vs_pool[:, :T].indirect(slots(g * PAGE, PAGE)), ACT.Copy)
+            vs_row = vs_rows[:, g * PAGE : (g + 1) * PAGE]
+            nc.scalar.activation(vs_row, vs_pool[:, :T].indirect(slots(g * PAGE, PAGE)), ACT.Copy)
             vs_turned.append(psum.tile([P, PACK, P], F32, name="vs_turned", tag="vs_turned%d" % g))
             for r in range(PACK):
                 nc.tensor.transpose(vs_turned[g][:, r, :], vs_row[:, r::PACK], ident[:])
@@ -130,9 +126,17 @@ def tile_attend_pkv8_rel2_gate_kernel(
                 kw[g][:].rearrange("p r s -> p s r"), kw_pool[:].bitcast(U32).indirect(slots(g * PAGE, PAGE))
             )
 
+        vsc_rows = keep.tile([P, PAGES * DV], U8, name="vsc_rows", align_bytes=64)
+        nc.vector.tensor_copy(vsc_rows[:], vsc_pool[:].indirect(val_list[:]))
+        vsc = keep.tile([P, PAGES * DV], U8, name="vsc", tag="vsc_pool", align_bytes=64)
+        place_scale_rows(vsc, vsc_rows, VSC_ROW0)
+
         steps = PAGES * BLOCKS
         scores = [psum.tile([P, PACK, P], F32, name="score", tag="score%d" % t) for t in range(steps)]
-        pos = [keep.tile([P, PACK, P], F32, name="pos", tag="pos%d" % t, align_bytes=64) for t in range(steps)]
+        pos = [
+            [keep.tile([P, PACK, HALF], F32, name="pos", tag="pos%d%s" % (t, half), align_bytes=64) for half in "ab"]
+            for t in range(steps)
+        ]
         weight = [keep.tile([P, PACK, P], F32, name="weight", tag="weight%d" % t, align_bytes=64) for t in range(steps)]
         w_bf = [keep.tile([P, NQ, PACK], BF16, name="w_bf", tag="w_bf%d" % g, align_bytes=64) for g in range(PAGES)]
         sums = [psum.tile([P, P], F32, name="sums", tag="sums%d" % h) for h in range(BLOCKS)]
@@ -153,16 +157,16 @@ def tile_attend_pkv8_rel2_gate_kernel(
                 )
 
         def rectify(t, cols):
-            nc.scalar.activation(pos[t][:, :, cols], scores[t][:, :, cols], ACT.Relu)
+            nc.scalar.activation(pos[t][cols.start // HALF][:], scores[t][:, :, cols], ACT.Relu)
 
         def rectify_vector(t, cols):
-            nc.vector.tensor_scalar(pos[t][:, :, cols], scores[t][:, :, cols], 0.0, None, ALU.max)
+            nc.vector.tensor_scalar(pos[t][cols.start // HALF][:], scores[t][:, :, cols], 0.0, None, ALU.max)
 
         def square(t, cols):
-            nc.scalar.activation(weight[t][:, :, cols], pos[t][:, :, cols], ACT.Square)
+            nc.scalar.activation(weight[t][:, :, cols], pos[t][cols.start // HALF][:], ACT.Square)
 
         def square_gpsimd(t, cols):
-            nc.gpsimd.tensor_tensor(weight[t][:, :, cols], pos[t][:, :, cols], pos[t][:, :, cols], ALU.mult)
+            nc.gpsimd.tensor_tensor(weight[t][:, :, cols], pos[t][cols.start // HALF][:], pos[t][cols.start // HALF][:], ALU.mult)
 
         def add_up(t):
             g, h = divmod(t, BLOCKS)
@@ -187,7 +191,7 @@ def tile_attend_pkv8_rel2_gate_kernel(
             )
 
         def quantise(g, first, count, tag):
-            codes = keep.tile([P, count], U32, name="w_codes", tag="codes_" + tag, align_bytes=64)
+            codes = keep.tile([P, count], U32, name="w_codes", tag=tag, align_bytes=64)
             scales = keep.tile([P, count], U8, name="w_scales", tag="scales_" + tag, align_bytes=64)
             nc.vector.quantize_mx(
                 out=codes[:].bitcast(FP8X4),
@@ -196,56 +200,47 @@ def tile_attend_pkv8_rel2_gate_kernel(
             )
             return codes, scales
 
-        rectify(0, high)
-        rectify(0, low)
-        square_gpsimd(0, high)
-        square(0, low)
         vw = keep.tile([P, PAGES * DV], U32, name="vw", align_bytes=64)
         nc.vector.tensor_copy(vw[:], vw_pool[:].bitcast(U32).indirect(val_list[:]))
-        rectify_vector(1, high)
-        rectify_vector(1, low)
-        square_gpsimd(1, high)
-        weigh(0, whole)
-        rectify(2, low)
-        rectify(2, high)
-        square(1, low)
-        weigh(1, whole)
-        square(2, whole)
-        weigh(2, whole)
-        rectify(3, low)
-        rectify(3, high)
-        square(3, low)
-        square(3, high)
-        first_codes, first_scales = quantise(0, 0, NQ, "first")
-        weigh(3, low)
-        weigh(3, high)
+        for t in range(steps - 1):
+            if t == 2:
+                rectify_vector(t, high)
+            else:
+                rectify(t, high)
+            rectify(t, low)
+            square_gpsimd(t, high)
+            square(t, low)
+            if t == steps - 2:
+                first_codes, first_scales = quantise(0, 0, NQ, "first")
+            weigh(t, whole)
+        for step in (rectify, square, weigh):
+            step(steps - 1, low)
+            step(steps - 1, high)
         for t in range(steps):
             add_up(t)
 
-        totals = []
-        for h in range(BLOCKS):
-            spare = keep.tile([P, P], F32, name="spare", tag="spare%d" % h)
-            total = keep.tile([P, 1], F32, name="total%d" % h)
-            nc.scalar.activation(spare[:], sums[h][:], ACT.Copy, bias=1.0 / P, accum_out=total[:])
-            totals.append(total)
-
         gate = keep.tile([P, BLOCKS, DV], F32, name="gate")
-        og_tanh = keep.tile([P, BLOCKS, DV], F32, name="og_tanh")
+        og_tanh = keep.tile([P, BLOCKS, DV], F32, name="og_tanh", tag="pos3a", align_bytes=64)
         nc.scalar.activation(og_tanh[:], og_raw[:], ACT.Tanh, scale=0.5)
-        nc.scalar.activation(gate[:], og_tanh[:], ACT.Copy, scale=0.5, bias=0.5)
-
+        totals = keep.tile([P, BLOCKS], F32, name="totals")
         for h in range(BLOCKS):
-            last_codes, last_scales = quantise(1, h * P, P, "last%d" % h)
-            inverse = keep.tile([P, 1], F32, name="inverse", tag="w_bf%d" % h, align_bytes=64)
-            nc.vector.reciprocal(inverse[:], totals[h][:])
-            acc = psum.tile([P, DV], F32, name="acc", tag="score%d" % h)
-            operands = [
-                (first_codes[:, h * P : (h + 1) * P], first_scales[:, h * P : (h + 1) * P]),
-                (last_codes[:], last_scales[:]),
-            ]
-            for g, (codes, scales) in enumerate(operands):
+            if h == BLOCKS - 1:
+                nc.scalar.activation(gate[:], og_tanh[:], ACT.Copy, scale=0.5, bias=0.5)
+            spare = keep.tile([P, P], F32, name="spare", tag="spare%d" % h)
+            nc.scalar.activation(spare[:], sums[h][:], ACT.Copy, bias=1.0 / P, accum_out=totals[:, h : h + 1])
+
+        last = [quantise(1, h * P, P, "last%d" % h) for h in range(BLOCKS)]
+        inverse = keep.tile([P, BLOCKS], F32, name="inverse")
+        nc.vector.reciprocal(inverse[:], totals[:])
+        acc = [psum.tile([P, DV], F32, name="acc", tag="score%d" % h) for h in range(BLOCKS)]
+        for g in range(PAGES):
+            for h in range(BLOCKS):
+                if g == 0:
+                    codes, scales = first_codes[:, h * P : (h + 1) * P], first_scales[:, h * P : (h + 1) * P]
+                else:
+                    codes, scales = last[h][0][:], last[h][1][:]
                 nc.tensor.matmul_mx(
-                    out=acc[:],
+                    out=acc[h][:],
                     lhsT=codes.bitcast(FP8X4),
                     lhsT_scale=scales,
                     rhs=vw[:, g * DV : (g + 1) * DV].bitcast(FP8X4),
@@ -253,6 +248,9 @@ def tile_attend_pkv8_rel2_gate_kernel(
                     start=(g == 0),
                     stop=(g == PAGES - 1),
                 )
+        for h in range(BLOCKS):
             result = keep.tile([P, DV], F32, name="result", tag="result%d" % h, align_bytes=64)
-            nc.vector.scalar_tensor_tensor(result[:], acc[:], inverse[:], gate[:, h, :], ALU.mult, ALU.mult)
+            nc.vector.scalar_tensor_tensor(
+                result[:], acc[h][:], inverse[:, h : h + 1], gate[:, h, :], ALU.mult, ALU.mult
+            )
             nc.sync.dma_start(out=out[0, h * P : (h + 1) * P, :], in_=result[:])

@@ -207,7 +207,10 @@ def tile_attend_pkv8_rel2_gate_kernel(
                 rectify_vector(t, high)
             else:
                 rectify(t, high)
-            rectify(t, low)
+            if t == 2:
+                rectify_vector(t, low)
+            else:
+                rectify(t, low)
             square_gpsimd(t, high)
             square(t, low)
             if t == steps - 2:

@@ -60,9 +60,9 @@ def tile_attend_pkv8_rel2_gate_kernel(
         make_identity(nc, ident[:], nomemset=True)
         nc.gpsimd.memset(vsc_words[:VSC_ROW0, :], 0)
 
-        nc.sync.dma_start(key_list[:], offs)
+        nc.scalar.dma_start(out=vs_pool[VS_ROW:, :T], in_=vs[0:1, :])
         nc.sync.dma_start(out=ks_words[KS_ROW0 : KS_ROW0 + SCALE_ROWS, : T // 4], in_=k_scales[0].bitcast(I32))
-        nc.sync.dma_start(out=vs_pool[VS_ROW:, :T], in_=vs[0:1, :])
+        nc.sync.dma_start(key_list[:], offs)
         nc.sync.dma_start(out=q_raw[:], in_=qT[0].rearrange("(p r) q -> p r q", r=PACK))
         nc.sync.dma_start(out=kw_pool[:], in_=k_words[0].rearrange("p t r -> p (t r)").bitcast(I32))
         nc.sync.dma_start(val_list[:], voffs)
@@ -116,9 +116,13 @@ def tile_attend_pkv8_rel2_gate_kernel(
         for g in range(PAGES):
             vs_row = vs_rows[:, g * PAGE : (g + 1) * PAGE]
             nc.scalar.activation(vs_row, vs_pool[:, :T].indirect(slots(g * PAGE, PAGE)), ACT.Copy)
-            vs_turned.append(psum.tile([P, PACK, P], F32, name="vs_turned", tag="vs_turned%d" % g))
+
+        def turn_vs(g, bank):
+            vs_turned.append(psum.tile([P, PACK, P], F32, name="vs_turned", tag=bank))
             for r in range(PACK):
-                nc.tensor.transpose(vs_turned[g][:, r, :], vs_row[:, r::PACK], ident[:])
+                nc.tensor.transpose(vs_turned[g][:, r, :], vs_rows[:, g * PAGE + r : (g + 1) * PAGE : PACK], ident[:])
+
+        turn_vs(0, "vs_turned")
 
         kw = [keep.tile([P, PACK, P], U32, name="kw", tag="kw%d" % g, align_bytes=64) for g in range(PAGES)]
         for g in range(PAGES):
@@ -211,6 +215,8 @@ def tile_attend_pkv8_rel2_gate_kernel(
                 rectify_vector(t, low)
             else:
                 rectify(t, low)
+            if t == 0:
+                turn_vs(1, "score0")
             square_gpsimd(t, high)
             square(t, low)
             if t == steps - 2:
@@ -235,7 +241,7 @@ def tile_attend_pkv8_rel2_gate_kernel(
         last = [quantise(1, h * P, P, "last%d" % h) for h in range(BLOCKS)]
         inverse = keep.tile([P, BLOCKS], F32, name="inverse")
         nc.vector.reciprocal(inverse[:], totals[:])
-        acc = [psum.tile([P, DV], F32, name="acc", tag="score%d" % h) for h in range(BLOCKS)]
+        acc = [psum.tile([P, DV], F32, name="acc", tag="score%d" % (BLOCKS + h)) for h in range(BLOCKS)]
         for g in range(PAGES):
             for h in range(BLOCKS):
                 if g == 0:

@@ -206,25 +206,29 @@ def tile_attend_pkv8_rel2_gate_kernel(
 
         vw = keep.tile([P, PAGES * DV], U32, name="vw", align_bytes=64)
         nc.vector.tensor_copy(vw[:], vw_pool[:].bitcast(U32).indirect(val_list[:]))
-        for t in range(steps - 1):
-            if t == 2:
-                rectify_vector(t, high)
-            else:
-                rectify(t, high)
-            if t == 2:
-                rectify_vector(t, low)
-            else:
-                rectify(t, low)
-            if t == 0:
-                turn_vs(1, "score0")
-            square_gpsimd(t, high)
-            square(t, low)
-            if t == steps - 2:
-                first_codes, first_scales = quantise(0, 0, NQ, "first")
-            weigh(t, whole)
-        for step in (rectify, square, weigh):
-            step(steps - 1, low)
-            step(steps - 1, high)
+        rectify(0, high)
+        rectify(0, low)
+        turn_vs(1, "score0")
+        square_gpsimd(0, high)
+        rectify(1, high)
+        rectify(1, low)
+        square_gpsimd(1, high)
+        square(0, low)
+        square(1, low)
+        rectify_vector(2, high)
+        square_gpsimd(2, high)
+        rectify(2, low)
+        rectify(3, high)
+        square_gpsimd(3, high)
+        square(2, low)
+        rectify(3, low)
+        square(3, low)
+        weigh(0, whole)
+        weigh(1, whole)
+        weigh(2, whole)
+        first_codes, first_scales = quantise(0, 0, NQ, "first")
+        weigh(3, high)
+        weigh(3, low)
         for t in range(steps):
             add_up(t)
 

@@ -99,7 +99,7 @@ def tile_attend_pkv8_rel2_gate_kernel(
         )
         nc.sync.dma_start(out=og_raw[:], in_=og[0].rearrange("(h p) e -> p h e", p=P))
 
-        q_bf = keep.tile([P, NQ, PACK], BF16, name="q_bf", align_bytes=64)
+        q_bf = keep.tile([P, NQ, PACK], BF16, name="q_bf", tag="q_bf", align_bytes=64)
         q_codes = keep.tile([P, NQ], U32, name="q_codes", align_bytes=64)
         q_scales = keep.tile([P, NQ], U8, name="q_scales", align_bytes=64)
         nc.scalar.activation(
@@ -111,18 +111,18 @@ def tile_attend_pkv8_rel2_gate_kernel(
             out=q_codes[:].bitcast(FP8X4), scales=q_scales[:], in_=q_bf[:].rearrange("p q r -> p (q r)")
         )
 
-        vs_turned = []
-        vs_rows = keep.tile([P, N], F32, name="vs_rows", tag="q_raw")
-        for g in range(PAGES):
-            vs_row = vs_rows[:, g * PAGE : (g + 1) * PAGE]
-            nc.scalar.activation(vs_row, vs_pool[:, :T].indirect(slots(g * PAGE, PAGE)), ACT.Copy)
-
-        def turn_vs(g, bank):
-            vs_turned.append(psum.tile([P, PACK, P], F32, name="vs_turned", tag=bank))
-            for r in range(PACK):
-                nc.tensor.transpose(vs_turned[g][:, r, :], vs_rows[:, g * PAGE + r : (g + 1) * PAGE : PACK], ident[:])
-
-        turn_vs(0, "vs_turned")
+        vs_turned = [psum.tile([P, PACK, P], F32, name="vs_turned", tag="vs_turned%d" % g) for g in range(PAGES)]
+        vs_row = keep.tile([P, PAGE], F32, name="vs_row", tag="q_raw")
+        nc.scalar.activation(vs_row[:], vs_pool[:, :T].indirect(slots(0, PAGE)), ACT.Copy)
+        vs_dealt = keep.tile([P, PACK, P], F32, name="vs_dealt", tag="q_bf", align_bytes=64)
+        nc.vector.tensor_copy(
+            vs_dealt[:].bitcast(U32).rearrange("p r s -> p s r"),
+            vs_pool[:].bitcast(U32)[:, :T].indirect(slots(PAGE, PAGE)),
+        )
+        for r in range(PACK):
+            nc.tensor.transpose(vs_turned[0][:, r, :], vs_row[:, r::PACK], ident[:])
+        for r in range(PACK):
+            nc.tensor.transpose(vs_turned[1][:, r, :], vs_dealt[:, r, :], ident[:])
 
         kw = [keep.tile([P, PACK, P], U32, name="kw", tag="kw%d" % g, align_bytes=64) for g in range(PAGES)]
         for g in range(PAGES):
@@ -208,7 +208,6 @@ def tile_attend_pkv8_rel2_gate_kernel(
         nc.vector.tensor_copy(vw[:], vw_pool[:].bitcast(U32).indirect(val_list[:]))
         rectify(0, high)
         rectify(0, low)
-        turn_vs(1, "score0")
         square_gpsimd(0, high)
         rectify(1, high)
         rectify(1, low)

@@ -215,8 +215,8 @@ def tile_attend_pkv8_rel2_gate_kernel(
         square(0, low)
         square(1, low)
         rectify_vector(2, high)
+        rectify_vector(2, low)
         square_gpsimd(2, high)
-        rectify(2, low)
         rectify(3, high)
         square_gpsimd(3, high)
         square(2, low)
@@ -225,14 +225,14 @@ def tile_attend_pkv8_rel2_gate_kernel(
         weigh(0, whole)
         weigh(1, whole)
         weigh(2, whole)
-        first_codes, first_scales = quantise(0, 0, NQ, "first")
-        weigh(3, high)
-        weigh(3, low)
+        packed = [quantise(0, 0, P, "pos2b")]
+        weigh(3, whole)
+        packed.append(quantise(0, P, P, "pos3a"))
         for t in range(steps):
             add_up(t)
 
         gate = keep.tile([P, BLOCKS, DV], F32, name="gate")
-        og_tanh = keep.tile([P, BLOCKS, DV], F32, name="og_tanh", tag="pos3a", align_bytes=64)
+        og_tanh = keep.tile([P, BLOCKS, DV], F32, name="og_tanh", tag="pos2a", align_bytes=64)
         nc.scalar.activation(og_tanh[:], og_raw[:], ACT.Tanh, scale=0.5)
         totals = keep.tile([P, BLOCKS], F32, name="totals")
         for h in range(BLOCKS):
@@ -241,20 +241,17 @@ def tile_attend_pkv8_rel2_gate_kernel(
             spare = keep.tile([P, P], F32, name="spare", tag="spare%d" % h)
             nc.scalar.activation(spare[:], sums[h][:], ACT.Copy, bias=1.0 / P, accum_out=totals[:, h : h + 1])
 
-        last = [quantise(1, h * P, P, "last%d" % h) for h in range(BLOCKS)]
+        packed = packed + [quantise(1, h * P, P, "last%d" % h) for h in range(BLOCKS)]
         inverse = keep.tile([P, BLOCKS], F32, name="inverse")
         nc.vector.reciprocal(inverse[:], totals[:])
         acc = [psum.tile([P, DV], F32, name="acc", tag="score%d" % (BLOCKS + h)) for h in range(BLOCKS)]
         for g in range(PAGES):
             for h in range(BLOCKS):
-                if g == 0:
-                    codes, scales = first_codes[:, h * P : (h + 1) * P], first_scales[:, h * P : (h + 1) * P]
-                else:
-                    codes, scales = last[h][0][:], last[h][1][:]
+                codes, scales = packed[g * BLOCKS + h]
                 nc.tensor.matmul_mx(
                     out=acc[h][:],
-                    lhsT=codes.bitcast(FP8X4),
-                    lhsT_scale=scales,
+                    lhsT=codes[:].bitcast(FP8X4),
+                    lhsT_scale=scales[:],
                     rhs=vw[:, g * DV : (g + 1) * DV].bitcast(FP8X4),
                     rhs_scale=vsc[:, g * DV : (g + 1) * DV],
                     start=(g == 0),

@@ -21,7 +21,7 @@ PAGE = 512
 PAGES = N // PAGE
 POOL_PAGES = T // PAGE
 BLOCKS = NQ // P
-HALF = P // 2
+HALF = PACK // 2
 LIST_STEP = 16
 SCALE_ROWS = 16
 VSC_ROW0 = P - SCALE_ROWS
@@ -138,13 +138,13 @@ def tile_attend_pkv8_rel2_gate_kernel(
         steps = PAGES * BLOCKS
         scores = [psum.tile([P, PACK, P], F32, name="score", tag="score%d" % t) for t in range(steps)]
         pos = [
-            [keep.tile([P, PACK, HALF], F32, name="pos", tag="pos%d%s" % (t, half), align_bytes=64) for half in "ab"]
+            [keep.tile([P, HALF, P], F32, name="pos", tag="pos%d%s" % (t, half), align_bytes=64) for half in "ab"]
             for t in range(steps)
         ]
         weight = [keep.tile([P, PACK, P], F32, name="weight", tag="weight%d" % t, align_bytes=64) for t in range(steps)]
-        w_bf = [keep.tile([P, NQ, PACK], BF16, name="w_bf", tag="w_bf%d" % g, align_bytes=64) for g in range(PAGES)]
+        w_bf = [keep.tile([P, P, PACK], BF16, name="w_bf", tag="w_bf%d" % t, align_bytes=64) for t in range(steps)]
         sums = [psum.tile([P, P], F32, name="sums", tag="sums%d" % h) for h in range(BLOCKS)]
-        low, high, whole = slice(0, HALF), slice(HALF, P), slice(0, P)
+        low, high, whole = slice(0, HALF), slice(HALF, PACK), slice(0, P)
 
         for t in range(steps):
             g, h = divmod(t, BLOCKS)
@@ -161,16 +161,16 @@ def tile_attend_pkv8_rel2_gate_kernel(
                 )
 
         def rectify(t, cols):
-            nc.scalar.activation(pos[t][cols.start // HALF][:], scores[t][:, :, cols], ACT.Relu)
+            nc.scalar.activation(pos[t][cols.start // HALF][:], scores[t][:, cols, :], ACT.Relu)
 
         def rectify_vector(t, cols):
-            nc.vector.tensor_scalar(pos[t][cols.start // HALF][:], scores[t][:, :, cols], 0.0, None, ALU.max)
+            nc.vector.tensor_scalar(pos[t][cols.start // HALF][:], scores[t][:, cols, :], 0.0, None, ALU.max)
 
         def square(t, cols):
-            nc.scalar.activation(weight[t][:, :, cols], pos[t][cols.start // HALF][:], ACT.Square)
+            nc.scalar.activation(weight[t][:, cols, :], pos[t][cols.start // HALF][:], ACT.Square)
 
         def square_gpsimd(t, cols):
-            nc.gpsimd.tensor_tensor(weight[t][:, :, cols], pos[t][cols.start // HALF][:], pos[t][cols.start // HALF][:], ALU.mult)
+            nc.gpsimd.tensor_tensor(weight[t][:, cols, :], pos[t][cols.start // HALF][:], pos[t][cols.start // HALF][:], ALU.mult)
 
         def add_up(t):
             g, h = divmod(t, BLOCKS)
@@ -188,19 +188,19 @@ def tile_attend_pkv8_rel2_gate_kernel(
             g, h = divmod(t, BLOCKS)
             pairs = (cols.stop - cols.start) // 2
             nc.vector.tensor_tensor(
-                w_bf[g][:, h * P + cols.start : h * P + cols.stop, :].rearrange("s (c i) r -> s c r i", i=2),
+                w_bf[t][:, cols, :].rearrange("s (c i) r -> s c r i", i=2),
                 weight[t][:, :, cols].rearrange("s r (c i) -> s c r i", i=2),
                 vs_turned[g][:, :, VS_ROW:].unsqueeze(1).to_broadcast([P, pairs, PACK, 2]),
                 ALU.mult,
             )
 
-        def quantise(g, first, count, tag):
-            codes = keep.tile([P, count], U32, name="w_codes", tag=tag, align_bytes=64)
-            scales = keep.tile([P, count], U8, name="w_scales", tag="scales_" + tag, align_bytes=64)
+        def quantise(t, tag):
+            codes = keep.tile([P, P], U32, name="w_codes", tag=tag, align_bytes=64)
+            scales = keep.tile([P, P], U8, name="w_scales", tag="scales_" + tag, align_bytes=64)
             nc.vector.quantize_mx(
                 out=codes[:].bitcast(FP8X4),
                 scales=scales[:],
-                in_=w_bf[g][:, first : first + count, :].rearrange("s q r -> s (q r)"),
+                in_=w_bf[t][:].rearrange("s q r -> s (q r)"),
             )
             return codes, scales
 
@@ -225,9 +225,9 @@ def tile_attend_pkv8_rel2_gate_kernel(
         weigh(0, whole)
         weigh(1, whole)
         weigh(2, whole)
-        packed = [quantise(0, 0, P, "pos2b")]
+        packed = [quantise(0, "pos2b")]
         weigh(3, whole)
-        packed.append(quantise(0, P, P, "pos3a"))
+        packed.append(quantise(1, "pos3a"))
         for t in range(steps):
             add_up(t)
 
@@ -241,8 +241,8 @@ def tile_attend_pkv8_rel2_gate_kernel(
             spare = keep.tile([P, P], F32, name="spare", tag="spare%d" % h)
             nc.scalar.activation(spare[:], sums[h][:], ACT.Copy, bias=1.0 / P, accum_out=totals[:, h : h + 1])
 
-        packed = packed + [quantise(1, h * P, P, "last%d" % h) for h in range(BLOCKS)]
-        inverse = keep.tile([P, BLOCKS], F32, name="inverse")
+        packed = packed + [quantise(BLOCKS + h, "last%d" % h) for h in range(BLOCKS)]
+        inverse = keep.tile([P, BLOCKS], F32, name="inverse", tag="w_bf1", align_bytes=64)
         nc.vector.reciprocal(inverse[:], totals[:])
         acc = [psum.tile([P, DV], F32, name="acc", tag="score%d" % (BLOCKS + h)) for h in range(BLOCKS)]
         for g in range(PAGES):

@@ -21,7 +21,7 @@ PAGE = 512
 PAGES = N // PAGE
 POOL_PAGES = T // PAGE
 BLOCKS = NQ // P
-HALF = PACK // 2
+CUTS = (3, 2, 2, 2)
 LIST_STEP = 16
 SCALE_ROWS = 16
 VSC_ROW0 = P - SCALE_ROWS
@@ -137,14 +137,21 @@ def tile_attend_pkv8_rel2_gate_kernel(
 
         steps = PAGES * BLOCKS
         scores = [psum.tile([P, PACK, P], F32, name="score", tag="score%d" % t) for t in range(steps)]
+        low = [slice(0, cut) for cut in CUTS]
+        high = [slice(cut, PACK) for cut in CUTS]
         pos = [
-            [keep.tile([P, HALF, P], F32, name="pos", tag="pos%d%s" % (t, half), align_bytes=64) for half in "ab"]
+            {
+                rows.start: keep.tile(
+                    [P, rows.stop - rows.start, P], F32, name="pos", tag="pos%d%s" % (t, part), align_bytes=64
+                )
+                for part, rows in (("a", low[t]), ("b", high[t]))
+            }
             for t in range(steps)
         ]
         weight = [keep.tile([P, PACK, P], F32, name="weight", tag="weight%d" % t, align_bytes=64) for t in range(steps)]
         w_bf = [keep.tile([P, P, PACK], BF16, name="w_bf", tag="w_bf%d" % t, align_bytes=64) for t in range(steps)]
         sums = [psum.tile([P, P], F32, name="sums", tag="sums%d" % h) for h in range(BLOCKS)]
-        low, high, whole = slice(0, HALF), slice(HALF, PACK), slice(0, P)
+        whole = slice(0, P)
 
         for t in range(steps):
             g, h = divmod(t, BLOCKS)
@@ -161,16 +168,16 @@ def tile_attend_pkv8_rel2_gate_kernel(
                 )
 
         def rectify(t, cols):
-            nc.scalar.activation(pos[t][cols.start // HALF][:], scores[t][:, cols, :], ACT.Relu)
+            nc.scalar.activation(pos[t][cols.start][:], scores[t][:, cols, :], ACT.Relu)
 
         def rectify_vector(t, cols):
-            nc.vector.tensor_scalar(pos[t][cols.start // HALF][:], scores[t][:, cols, :], 0.0, None, ALU.max)
+            nc.vector.tensor_scalar(pos[t][cols.start][:], scores[t][:, cols, :], 0.0, None, ALU.max)
 
         def square(t, cols):
-            nc.scalar.activation(weight[t][:, cols, :], pos[t][cols.start // HALF][:], ACT.Square)
+            nc.scalar.activation(weight[t][:, cols, :], pos[t][cols.start][:], ACT.Square)
 
         def square_gpsimd(t, cols):
-            nc.gpsimd.tensor_tensor(weight[t][:, cols, :], pos[t][cols.start // HALF][:], pos[t][cols.start // HALF][:], ALU.mult)
+            nc.gpsimd.tensor_tensor(weight[t][:, cols, :], pos[t][cols.start][:], pos[t][cols.start][:], ALU.mult)
 
         def add_up(t):
             g, h = divmod(t, BLOCKS)
@@ -206,22 +213,22 @@ def tile_attend_pkv8_rel2_gate_kernel(
 
         vw = keep.tile([P, PAGES * DV], U32, name="vw", align_bytes=64)
         nc.vector.tensor_copy(vw[:], vw_pool[:].bitcast(U32).indirect(val_list[:]))
-        rectify(0, high)
-        rectify(0, low)
-        square_gpsimd(0, high)
-        rectify(1, high)
-        rectify(1, low)
-        square_gpsimd(1, high)
-        square(0, low)
-        square(1, low)
-        rectify_vector(2, high)
-        rectify_vector(2, low)
-        square_gpsimd(2, high)
-        rectify(3, high)
-        square_gpsimd(3, high)
-        square(2, low)
-        rectify(3, low)
-        square(3, low)
+        rectify(0, high[0])
+        rectify(0, low[0])
+        square_gpsimd(0, high[0])
+        rectify(1, high[1])
+        rectify(1, low[1])
+        square_gpsimd(1, high[1])
+        square(0, low[0])
+        square(1, low[1])
+        rectify_vector(2, high[2])
+        rectify_vector(2, low[2])
+        square_gpsimd(2, high[2])
+        rectify(3, high[3])
+        square_gpsimd(3, high[3])
+        square(2, low[2])
+        rectify(3, low[3])
+        square(3, low[3])
         weigh(0, whole)
         weigh(1, whole)
         weigh(2, whole)

from contextlib import ExitStack

import concourse.mybir as mybir
from concourse.masks import make_identity

F32 = mybir.dt.float32
BF16 = mybir.dt.bfloat16
I32 = mybir.dt.int32
U32 = mybir.dt.uint32
U16 = mybir.dt.uint16
U8 = mybir.dt.uint8
FP8X4 = mybir.dt.float8_e4m3fn_x4
ACT = mybir.ActivationFunctionType
ALU = mybir.AluOpType

P = 128
PACK = 4
QUADS = 4
N, T, D, DV, NQ = 1024, 4096, 512, 128, 256
PAGE = 512
PAGES = N // PAGE
POOL_PAGES = T // PAGE
BLOCKS = NQ // P
CUTS = (3, 2, 2, 2)
LIST_STEP = 16
SCALE_ROWS = 16
VSC_ROW0 = P - SCALE_ROWS
KS_ROW0 = 48
VS_ROW = P - 1
VS_SPLIT = 2944

FLOPS = 2 * NQ * N * D + 2 * NQ * N * DV


def tile_attend_pkv8_rel2_gate_kernel(
    tc, qT, k_words, k_scales, v_words, v_scales, vs, og, offs, voffs, out
):
    nc = tc.nc
    with ExitStack() as ctx:
        keep = ctx.enter_context(tc.tile_pool(name="keep", bufs=1))
        shared = ctx.enter_context(tc.tile_pool(name="shared", bufs=1))
        psum = ctx.enter_context(tc.psum_pool(name="psum", bufs=1))

        key_list = keep.tile([P, N // LIST_STEP], U16, name="key_list")
        val_list = keep.tile([P, PAGES * DV // LIST_STEP], U16, name="val_list")
        kw_pool = keep.tile([P, T], I32, name="kw_pool", align_bytes=64)
        ks_pool = shared.tile([P, T + 4], U8, name="ks_pool", align_bytes=64, offset=0)
        vsc_pool = keep.tile([P, POOL_PAGES * DV], U8, name="vsc_pool", tag="vsc_pool", align_bytes=64)
        vs_pool = keep.tile([P, T + 1], F32, name="vs_pool", align_bytes=64)
        q_raw = keep.tile([P, PACK, NQ], F32, name="q_raw", tag="q_raw")
        ident = keep.tile([P, P], F32, name="ident")

        ks_words = ks_pool[:].bitcast(I32)
        vsc_words = vsc_pool[:].bitcast(I32)
        nc.vector.memset(ks_words[:KS_ROW0, :], 0)
        nc.gpsimd.memset(ks_words[KS_ROW0 + SCALE_ROWS :, :], 0)
        nc.vector.memset(vs_pool[:VS_ROW, VS_SPLIT:], 0.0)
        nc.gpsimd.memset(vs_pool[:VS_ROW, :VS_SPLIT], 0.0)
        nc.gpsimd.memset(ident[:], 0.0)
        make_identity(nc, ident[:], nomemset=True)
        nc.gpsimd.memset(vsc_words[:VSC_ROW0, :], 0)

        nc.scalar.dma_start(out=vs_pool[VS_ROW:, :T], in_=vs[0:1, :])
        nc.sync.dma_start(out=ks_words[KS_ROW0 : KS_ROW0 + SCALE_ROWS, : T // 4], in_=k_scales[0].bitcast(I32))
        nc.sync.dma_start(key_list[:], offs)
        nc.sync.dma_start(out=q_raw[:], in_=qT[0].rearrange("(p r) q -> p r q", r=PACK))
        nc.sync.dma_start(out=kw_pool[:], in_=k_words[0].rearrange("p t r -> p (t r)").bitcast(I32))
        nc.sync.dma_start(val_list[:], voffs)
        nc.sync.dma_start(
            out=vsc_words[VSC_ROW0:, :].rearrange("f (u e) -> f u e", u=POOL_PAGES),
            in_=v_scales.rearrange("u f e -> f u e").bitcast(I32),
        )

        def slots(first, count):
            return key_list[:, first // LIST_STEP : (first + count) // LIST_STEP]

        def place_scale_rows(plane, gathered, row0):
            for quad in range(QUADS):
                first = row0 + 4 * quad
                nc.sync.dma_start(
                    out=plane[32 * quad : 32 * quad + 4, :].bitcast(I32),
                    in_=gathered[first : first + 4, :].bitcast(I32),
                )

        ks_rows = shared.tile([P, N], U8, name="ks_rows", align_bytes=64, offset=4160)
        nc.vector.tensor_copy(ks_rows[:], ks_pool[:, :T].indirect(key_list[:]))
        ks_dealt = keep.tile([P, N], U8, name="ks_dealt", tag="ks_dealt", align_bytes=64)
        nc.vector.tensor_copy(
            ks_dealt[:].rearrange("p (g r s) -> p g s r", g=PAGES, r=PACK),
            ks_rows[:].rearrange("p (g s r) -> p g s r", g=PAGES, r=PACK),
        )
        ks = shared.tile([P, N], U8, name="ks", align_bytes=64, offset=1024)
        place_scale_rows(ks, ks_dealt, KS_ROW0)
        og_raw = shared.tile([P, BLOCKS, DV], F32, name="og_raw", align_bytes=64, offset=3648)
        vw_pool = shared.tile([P, POOL_PAGES * DV], I32, name="vw_pool", align_bytes=64, offset=4672)
        nc.sync.dma_start(
            out=vw_pool[:].rearrange("p (u e) -> p u e", u=POOL_PAGES),
            in_=v_words.rearrange("u p e r -> p u (e r)").bitcast(I32),
        )
        nc.sync.dma_start(out=og_raw[:], in_=og[0].rearrange("(h p) e -> p h e", p=P))

        q_bf = keep.tile([P, NQ, PACK], BF16, name="q_bf", tag="q_bf", align_bytes=64)
        q_codes = keep.tile([P, NQ], U32, name="q_codes", align_bytes=64)
        q_scales = keep.tile([P, NQ], U8, name="q_scales", align_bytes=64)
        nc.scalar.activation(
            q_bf[:].rearrange("p (c i) r -> p c r i", i=4),
            q_raw[:].rearrange("p r (c i) -> p c r i", i=4),
            ACT.Copy,
        )
        nc.vector.quantize_mx(
            out=q_codes[:].bitcast(FP8X4), scales=q_scales[:], in_=q_bf[:].rearrange("p q r -> p (q r)")
        )

        vs_turned = [psum.tile([P, PACK, P], F32, name="vs_turned", tag="vs_turned%d" % g) for g in range(PAGES)]
        vs_row = keep.tile([P, PAGE], F32, name="vs_row", tag="q_raw")
        nc.scalar.activation(vs_row[:], vs_pool[:, :T].indirect(slots(0, PAGE)), ACT.Copy)
        vs_dealt = keep.tile([P, PACK, P], F32, name="vs_dealt", tag="q_bf", align_bytes=64)
        nc.vector.tensor_copy(
            vs_dealt[:].bitcast(U32).rearrange("p r s -> p s r"),
            vs_pool[:].bitcast(U32)[:, :T].indirect(slots(PAGE, PAGE)),
        )
        for r in range(PACK):
            nc.tensor.transpose(vs_turned[0][:, r, :], vs_row[:, r::PACK], ident[:])
        for r in range(PACK):
            nc.tensor.transpose(vs_turned[1][:, r, :], vs_dealt[:, r, :], ident[:])

        kw = [keep.tile([P, PACK, P], U32, name="kw", tag="kw%d" % g, align_bytes=64) for g in range(PAGES)]
        for g in range(PAGES):
            nc.vector.tensor_copy(
                kw[g][:].rearrange("p r s -> p s r"), kw_pool[:].bitcast(U32).indirect(slots(g * PAGE, PAGE))
            )

        vsc_rows = keep.tile([P, PAGES * DV], U8, name="vsc_rows", align_bytes=64)
        nc.vector.tensor_copy(vsc_rows[:], vsc_pool[:].indirect(val_list[:]))
        vsc = keep.tile([P, PAGES * DV], U8, name="vsc", tag="vsc_pool", align_bytes=64)
        place_scale_rows(vsc, vsc_rows, VSC_ROW0)

        steps = PAGES * BLOCKS
        scores = [psum.tile([P, PACK, P], F32, name="score", tag="score%d" % t) for t in range(steps)]
        low = [slice(0, cut) for cut in CUTS]
        high = [slice(cut, PACK) for cut in CUTS]
        pos = [
            {
                rows.start: keep.tile(
                    [P, rows.stop - rows.start, P], F32, name="pos", tag="pos%d%s" % (t, part), align_bytes=64
                )
                for part, rows in (("a", low[t]), ("b", high[t]))
            }
            for t in range(steps)
        ]
        weight = [keep.tile([P, PACK, P], F32, name="weight", tag="weight%d" % t, align_bytes=64) for t in range(steps)]
        w_bf = [keep.tile([P, P, PACK], BF16, name="w_bf", tag="w_bf%d" % t, align_bytes=64) for t in range(steps)]
        sums = [psum.tile([P, P], F32, name="sums", tag="sums%d" % h) for h in range(BLOCKS)]
        whole = slice(0, P)

        for t in range(steps):
            g, h = divmod(t, BLOCKS)
            for r in range(PACK):
                first = g * PAGE + r * P
                nc.tensor.matmul_mx(
                    out=scores[t][:, r, :],
                    lhsT=kw[g][:, r, :].bitcast(FP8X4),
                    lhsT_scale=ks[:, first : first + P],
                    rhs=q_codes[:, h * P : (h + 1) * P].bitcast(FP8X4),
                    rhs_scale=q_scales[:, h * P : (h + 1) * P],
                    start=True,
                    stop=True,
                )

        def rectify(t, cols):
            nc.scalar.activation(pos[t][cols.start][:], scores[t][:, cols, :], ACT.Relu)

        def rectify_vector(t, cols):
            nc.vector.tensor_scalar(pos[t][cols.start][:], scores[t][:, cols, :], 0.0, None, ALU.max)

        def square(t, cols):
            nc.scalar.activation(weight[t][:, cols, :], pos[t][cols.start][:], ACT.Square)

        def square_gpsimd(t, cols):
            nc.gpsimd.tensor_tensor(weight[t][:, cols, :], pos[t][cols.start][:], pos[t][cols.start][:], ALU.mult)

        def add_up(t):
            g, h = divmod(t, BLOCKS)
            for r in range(PACK):
                nc.tensor.matmul(
                    sums[h][:],
                    weight[t][:, r, :],
                    ident[:],
                    start=(g == 0 and r == 0),
                    stop=(g == PAGES - 1 and r == PACK - 1),
                    is_transpose=True,
                )

        def weigh(t, cols):
            g, h = divmod(t, BLOCKS)
            pairs = (cols.stop - cols.start) // 2
            nc.vector.tensor_tensor(
                w_bf[t][:, cols, :].rearrange("s (c i) r -> s c r i", i=2),
                weight[t][:, :, cols].rearrange("s r (c i) -> s c r i", i=2),
                vs_turned[g][:, :, VS_ROW:].unsqueeze(1).to_broadcast([P, pairs, PACK, 2]),
                ALU.mult,
            )

        def quantise(t, tag):
            codes = keep.tile([P, P], U32, name="w_codes", tag=tag, align_bytes=64)
            scales = keep.tile([P, P], U8, name="w_scales", tag="scales_" + tag, align_bytes=64)
            nc.vector.quantize_mx(
                out=codes[:].bitcast(FP8X4),
                scales=scales[:],
                in_=w_bf[t][:].rearrange("s q r -> s (q r)"),
            )
            return codes, scales

        vw = keep.tile([P, PAGES * DV], U32, name="vw", align_bytes=64)
        nc.vector.tensor_copy(vw[:], vw_pool[:].bitcast(U32).indirect(val_list[:]))
        rectify(0, high[0])
        rectify(0, low[0])
        square_gpsimd(0, high[0])
        rectify(1, high[1])
        rectify(1, low[1])
        square_gpsimd(1, high[1])
        square(0, low[0])
        square(1, low[1])
        rectify_vector(2, high[2])
        rectify_vector(2, low[2])
        square_gpsimd(2, high[2])
        rectify(3, high[3])
        square_gpsimd(3, high[3])
        square(2, low[2])
        rectify(3, low[3])
        square(3, low[3])
        weigh(0, whole)
        weigh(1, whole)
        weigh(2, whole)
        packed = [quantise(0, "pos2b")]
        weigh(3, whole)
        packed.append(quantise(1, "pos3a"))
        for t in range(steps):
            add_up(t)

        gate = keep.tile([P, BLOCKS, DV], F32, name="gate")
        og_tanh = keep.tile([P, BLOCKS, DV], F32, name="og_tanh", tag="pos2a", align_bytes=64)
        nc.scalar.activation(og_tanh[:], og_raw[:], ACT.Tanh, scale=0.5)
        totals = keep.tile([P, BLOCKS], F32, name="totals")
        for h in range(BLOCKS):
            if h == BLOCKS - 1:
                nc.scalar.activation(gate[:], og_tanh[:], ACT.Copy, scale=0.5, bias=0.5)
            spare = keep.tile([P, P], F32, name="spare", tag="spare%d" % h)
            nc.scalar.activation(spare[:], sums[h][:], ACT.Copy, bias=1.0 / P, accum_out=totals[:, h : h + 1])

        packed = packed + [quantise(BLOCKS + h, "last%d" % h) for h in range(BLOCKS)]
        inverse = keep.tile([P, BLOCKS], F32, name="inverse", tag="w_bf1", align_bytes=64)
        nc.vector.reciprocal(inverse[:], totals[:])
        acc = [psum.tile([P, DV], F32, name="acc", tag="score%d" % (BLOCKS + h)) for h in range(BLOCKS)]
        for g in range(PAGES):
            for h in range(BLOCKS):
                codes, scales = packed[g * BLOCKS + h]
                nc.tensor.matmul_mx(
                    out=acc[h][:],
                    lhsT=codes[:].bitcast(FP8X4),
                    lhsT_scale=scales[:],
                    rhs=vw[:, g * DV : (g + 1) * DV].bitcast(FP8X4),
                    rhs_scale=vsc[:, g * DV : (g + 1) * DV],
                    start=(g == 0),
                    stop=(g == PAGES - 1),
                )
        for h in range(BLOCKS):
            result = keep.tile([P, DV], F32, name="result", tag="result%d" % h, align_bytes=64)
            nc.vector.scalar_tensor_tensor(
                result[:], acc[h][:], inverse[:, h : h + 1], gate[:, h, :], ALU.mult, ALU.mult
            )
            nc.sync.dma_start(out=out[0, h * P : (h + 1) * P, :], in_=result[:])
